import numpy as np
import ml_dtypes


def mxq(x, axis, fmt="e4m3"):
    dtype, down = {"e4m3": (ml_dtypes.float8_e4m3fn, 7), "e5m2": (ml_dtypes.float8_e5m2, 14)}[fmt]
    v = np.moveaxis(np.asarray(x, np.float32).astype(ml_dtypes.bfloat16).astype(np.float64), axis, -1)
    blocks = v.reshape(v.shape[:-1] + (-1, 32))
    amax = np.abs(blocks).max(-1, keepdims=True)
    byte = np.maximum(np.where(amax > 0, np.frexp(amax)[1] - 1 + 127, 0) - down, 1)
    scale = np.exp2(byte - 127.0)
    codes = (blocks / scale).astype(np.float32).astype(dtype).astype(np.float64)
    return np.moveaxis((codes * scale).reshape(v.shape), -1, axis)


WIDE = False


def mx_kscale(k):
    if not WIDE:
        return np.ones(k)
    levels = np.array([10, -10, 5, -5, 0])
    if k % 512:
        return np.exp2(np.random.permutation(np.resize(levels, k // 32))).repeat(32)
    a = np.empty((k // 512, 16))
    for p in range(k // 512):
        a[p, :8] = np.random.permutation(np.resize(levels, 8))
        for g in range(8):
            far = levels[np.abs(levels - a[p, g]) >= 10]
            a[p, g + 8] = far[np.random.randint(len(far))]
    return np.exp2(a.ravel()).repeat(32)


def f64(x):
    return np.asarray(x).astype(np.float64)


def striped(idx):
    return np.tile(idx.reshape(-1, 16).T, (8, 1)).astype(np.uint16)


def unstriped(offs):
    return offs[:16].T.reshape(-1).astype(np.int64)


def pack_weight(w):
    k, n = w.shape
    w = f64(np.asarray(w, np.float32).astype(ml_dtypes.bfloat16)).reshape(k // 32, 32, n)
    amax = np.abs(w).max(1)
    byte = np.clip(np.where(amax > 0, np.frexp(amax)[1] - 1 + 127 - 7, 1), 1, 254)
    scaled = (w * np.exp2(127.0 - byte)[:, None, :]).reshape(k, n).astype(np.float32)
    words = np.ascontiguousarray(scaled.reshape(k // 512, 128, 4, n).transpose(0, 1, 3, 2)).astype(ml_dtypes.float8_e4m3fn).view(np.uint8)
    return words, np.ascontiguousarray(byte.astype(np.uint8).reshape(k // 512, 16, n))


def unpack_weight(words, scales):
    g, p, n, _ = words.shape
    vals = np.ascontiguousarray(words).view(ml_dtypes.float8_e4m3fn).astype(np.float64) * np.repeat(np.exp2(scales.astype(np.float64) - 127.0), 8, axis=1)[..., None]
    return vals.transpose(0, 1, 3, 2).reshape(g * 512, n)


K, T, S, N, U = 512, 4096, 1024, 256, 2048
P = 2 ** 7


def setup_inputs():
    n = np.random.standard_normal
    s = mx_kscale(K)[:, None]
    packed_xT = pack_weight(n((K, T)) * s)
    return {
        "x_words": packed_xT[0],
        "x_scales": packed_xT[1],
        "gate": np.tile(np.random.uniform(0.5, 1.5, S), (P, 1)).astype(np.float32),
        "w1": (n((K, N)) / np.sqrt(K) / s).astype(np.float32),
        "offs": striped(np.random.permutation(T)[:S]),
        "dst": striped(np.random.permutation(U)[:S]),
    }


def reference(x_words, x_scales, gate, w1, offs, dst):
    xq = unpack_weight(x_words, x_scales)[:, unstriped(offs)]
    y = mxq(f64(w1), 0, "e4m3").T @ xq
    out = np.zeros((N, U))
    out[:, unstriped(dst)] = y * f64(gate)[:1]
    return out

@@ -1,0 +1,104 @@
+from contextlib import ExitStack
+
+import concourse.mybir as mybir
+
+K, T, S, N, U = 512, 4096, 1024, 256, 2048
+P = 128
+PACK = 4
+FLOPS = 2 * K * N * S
+
+F32 = mybir.dt.float32
+BF16 = mybir.dt.bfloat16
+I32 = mybir.dt.int32
+U32 = mybir.dt.uint32
+U16 = mybir.dt.uint16
+U8 = mybir.dt.uint8
+FP8X4 = mybir.dt.float8_e4m3fn_x4
+MULT = mybir.AluOpType.mult
+
+
+def tile_picked_route2_linnone_p_kernel(tc, x_words, x_scales, gate, w1, offs, dst, out):
+    nc = tc.nc
+    with ExitStack() as ctx:
+        keep = ctx.enter_context(tc.tile_pool(name="keep", bufs=1))
+        psum = ctx.enter_context(tc.psum_pool(name="psum", bufs=1))
+
+        offs_sb = keep.tile([P, S // 16], U16, name="offs_sb")
+        dst_sb = keep.tile([P, S // 16], U16, name="dst_sb")
+        words = keep.tile([P, T], I32, name="words", align_bytes=64)
+        scales = keep.tile([P, T], U8, name="scales", tag="bytes_then_codes", align_bytes=64)
+        windows = [keep.tile([P, U], F32, name=f"window{b}") for b in range(2)]
+
+        nc.vector.memset(scales[:].bitcast(I32), 0)
+        nc.sync.dma_start(offs_sb[:], offs)
+
+        w_rows = w1.rearrange("(p j) m -> p j m", j=PACK)
+
+        def load_weights(b):
+            raw = keep.tile([P, PACK, P], F32, name=f"w_raw{b}", tag=f"stage{b}")
+            nc.sync.dma_start(raw[:], w_rows[:, :, b * P:(b + 1) * P])
+            grouped = keep.tile([P, P, PACK], BF16, name=f"w_grouped{b}", align_bytes=64)
+            nc.scalar.copy(grouped[:], raw[:].rearrange("p j m -> p m j"))
+            return grouped
+
+        def quantize_weights(b, grouped):
+            codes = keep.tile([P, P], U32, name=f"w_codes{b}", align_bytes=64)
+            plane = keep.tile([P, P], U8, name=f"w_plane{b}", align_bytes=64)
+            nc.vector.quantize_mx(out=codes[:].bitcast(FP8X4), scales=plane[:], in_=grouped[:].rearrange("p m j -> p (m j)"))
+            return codes, plane
+
+        grouped0 = load_weights(0)
+        nc.sync.dma_start(words[:], x_words[0].rearrange("p c t -> p (c t)").bitcast(I32))
+        for r in range(4):
+            nc.scalar.dma_start(scales[r:P:32, :].bitcast(I32), x_scales[0, r:16:4, :].bitcast(I32))
+        for b in range(2):
+            nc.vector.memset(windows[b][:], 0.0)
+        nc.sync.dma_start(dst_sb[:], dst)
+        grouped1 = load_weights(1)
+        gate_sb = keep.tile([P, S], F32, name="gate_sb", tag="stage0")
+        nc.sync.dma_start(gate_sb[:], gate)
+
+        weights0 = quantize_weights(0, grouped0)
+        x_plane = keep.tile([P, S], U8, name="x_plane", align_bytes=64)
+        nc.vector.tensor_copy(x_plane[:], scales[:].indirect(offs_sb[:]))
+        x_codes = keep.tile([P, S], U32, name="x_codes", tag="bytes_then_codes", align_bytes=64)
+
+        def gather_words(h):
+            nc.vector.tensor_copy(x_codes[:, 512 * h:512 * (h + 1)], words[:].bitcast(U32).indirect(offs_sb[:, 32 * h:32 * (h + 1)]))
+
+        def product(weights, lo, hi, y, y0):
+            codes, plane = weights
+            acc = psum.tile([P, hi - lo], F32, name="acc", tag="acc", bufs=4)
+            nc.tensor.matmul_mx(
+                out=acc[:],
+                lhsT=codes[:].bitcast(FP8X4),
+                lhsT_scale=plane[:],
+                rhs=x_codes[:, lo:hi].bitcast(FP8X4),
+                rhs_scale=x_plane[:, lo:hi],
+                start=True,
+                stop=True,
+            )
+            nc.scalar.copy(y[:, lo - y0:hi - y0], acc[:])
+
+        def scatter(b, lo, hi, y):
+            nc.vector.tensor_tensor(windows[b][:].indirect(dst_sb[:, lo // 16:hi // 16]), y[:], gate_sb[:, lo:hi], MULT)
+
+        gather_words(0)
+        gather_words(1)
+        weights1 = quantize_weights(1, grouped1)
+
+        y_head = keep.tile([P, 256], F32, name="y_head")
+        product(weights0, 0, 256, y_head, 0)
+        scatter(0, 0, 256, y_head)
+        y_rest = keep.tile([P, 768], F32, name="y_rest")
+        product(weights0, 256, 512, y_rest, 256)
+        product(weights0, 512, 1024, y_rest, 256)
+
+        scatter(0, 256, 1024, y_rest)
+        nc.sync.dma_start(out[0:P, :], windows[0][:])
+
+        y_second = keep.tile([P, S], F32, name="y_second")
+        product(weights1, 0, 512, y_second, 0)
+        product(weights1, 512, 1024, y_second, 0)
+        scatter(1, 0, 1024, y_second)
+        nc.sync.dma_start(out[P:2 * P, :], windows[1][:])

@@ -6,6 +6,8 @@ K, T, S, N, U = 512, 4096, 1024, 256, 2048
 P = 128
 PACK = 4
 FLOPS = 2 * K * N * S
+HEAD = 256
+SEED = 64
 
 F32 = mybir.dt.float32
 BF16 = mybir.dt.bfloat16
@@ -25,54 +27,47 @@ def tile_picked_route2_linnone_p_kernel(tc, x_words, x_scales, gate, w1, offs, d
 
         offs_sb = keep.tile([P, S // 16], U16, name="offs_sb")
         dst_sb = keep.tile([P, S // 16], U16, name="dst_sb")
-        words = keep.tile([P, T], I32, name="words", align_bytes=64)
         scales = keep.tile([P, T], U8, name="scales", tag="bytes_then_codes", align_bytes=64)
         windows = [keep.tile([P, U], F32, name=f"window{b}") for b in range(2)]
+        w_raw = keep.tile([P, PACK, N], F32, name="w_raw", tag="weights_then_gate")
 
+        zeros = keep.tile([P, SEED], F32, name="zeros", tag="zeros_then_words", align_bytes=64)
+        nc.vector.memset(zeros[:], 0.0)
         nc.vector.memset(scales[:].bitcast(I32), 0)
+        nc.sync.dma_start(w_raw[:], w1.rearrange("(p j) m -> p j m", j=PACK))
         nc.sync.dma_start(offs_sb[:], offs)
-
-        w_rows = w1.rearrange("(p j) m -> p j m", j=PACK)
-
-        def load_weights(b):
-            raw = keep.tile([P, PACK, P], F32, name=f"w_raw{b}", tag=f"stage{b}")
-            nc.sync.dma_start(raw[:], w_rows[:, :, b * P:(b + 1) * P])
-            grouped = keep.tile([P, P, PACK], BF16, name=f"w_grouped{b}", align_bytes=64)
-            nc.scalar.copy(grouped[:], raw[:].rearrange("p j m -> p m j"))
-            return grouped
-
-        def quantize_weights(b, grouped):
-            codes = keep.tile([P, P], U32, name=f"w_codes{b}", align_bytes=64)
-            plane = keep.tile([P, P], U8, name=f"w_plane{b}", align_bytes=64)
-            nc.vector.quantize_mx(out=codes[:].bitcast(FP8X4), scales=plane[:], in_=grouped[:].rearrange("p m j -> p (m j)"))
-            return codes, plane
-
-        grouped0 = load_weights(0)
-        nc.sync.dma_start(words[:], x_words[0].rearrange("p c t -> p (c t)").bitcast(I32))
-        for r in range(4):
-            nc.scalar.dma_start(scales[r:P:32, :].bitcast(I32), x_scales[0, r:16:4, :].bitcast(I32))
-        for b in range(2):
-            nc.vector.memset(windows[b][:], 0.0)
         nc.sync.dma_start(dst_sb[:], dst)
-        grouped1 = load_weights(1)
-        gate_sb = keep.tile([P, S], F32, name="gate_sb", tag="stage0")
+        for r in range(4):
+            nc.sync.dma_start(scales[r:P:32, :].bitcast(I32), x_scales[0, r:16:4, :].bitcast(I32))
+
+        nc.vector.tensor_copy(windows[0][:, 0:SEED], zeros[:])
+        words = keep.tile([P, T], I32, name="words", tag="zeros_then_words", align_bytes=64)
+        nc.sync.dma_start(words[:], x_words[0].rearrange("p c t -> p (c t)").bitcast(I32))
+        nc.vector.memset(windows[0][:, SEED:U], 0.0)
+        nc.scalar.copy(windows[1][:].rearrange("p (a c) -> p a c", c=SEED), windows[0][:, 0:SEED].unsqueeze(1).to_broadcast([P, U // SEED, SEED]))
+
+        w_grouped = keep.tile([P, N, PACK], BF16, name="w_grouped", align_bytes=64)
+        nc.scalar.copy(w_grouped[:], w_raw[:].rearrange("p j m -> p m j"))
+        gate_sb = keep.tile([P, S], F32, name="gate_sb", tag="weights_then_gate")
         nc.sync.dma_start(gate_sb[:], gate)
 
-        weights0 = quantize_weights(0, grouped0)
         x_plane = keep.tile([P, S], U8, name="x_plane", align_bytes=64)
         nc.vector.tensor_copy(x_plane[:], scales[:].indirect(offs_sb[:]))
-        x_codes = keep.tile([P, S], U32, name="x_codes", tag="bytes_then_codes", align_bytes=64)
 
-        def gather_words(h):
+        w_codes = keep.tile([P, N], U32, name="w_codes", align_bytes=64)
+        w_plane = keep.tile([P, N], U8, name="w_plane", align_bytes=64)
+        nc.vector.quantize_mx(out=w_codes[:].bitcast(FP8X4), scales=w_plane[:], in_=w_grouped[:].rearrange("p m j -> p (m j)"))
+
+        x_codes = keep.tile([P, S], U32, name="x_codes", tag="bytes_then_codes", align_bytes=64)
+        for h in range(2):
             nc.vector.tensor_copy(x_codes[:, 512 * h:512 * (h + 1)], words[:].bitcast(U32).indirect(offs_sb[:, 32 * h:32 * (h + 1)]))
 
-        def product(weights, lo, hi, y, y0):
-            codes, plane = weights
-            acc = psum.tile([P, hi - lo], F32, name="acc", tag="acc", bufs=4)
+        def product(b, lo, hi, y, y0):
+            acc = psum.tile([P, hi - lo], F32, name="acc", tag="acc", bufs=5)
             nc.tensor.matmul_mx(
                 out=acc[:],
-                lhsT=codes[:].bitcast(FP8X4),
-                lhsT_scale=plane[:],
+                lhsT=w_codes[:, b * P:(b + 1) * P].bitcast(FP8X4),
+                lhsT_scale=w_plane[:, b * P:(b + 1) * P],
                 rhs=x_codes[:, lo:hi].bitcast(FP8X4),
                 rhs_scale=x_plane[:, lo:hi],
                 start=True,
@@ -83,22 +78,17 @@ def tile_picked_route2_linnone_p_kernel(tc, x_words, x_scales, gate, w1, offs, d
         def scatter(b, lo, hi, y):
             nc.vector.tensor_tensor(windows[b][:].indirect(dst_sb[:, lo // 16:hi // 16]), y[:], gate_sb[:, lo:hi], MULT)
 
-        gather_words(0)
-        gather_words(1)
-        weights1 = quantize_weights(1, grouped1)
-
-        y_head = keep.tile([P, 256], F32, name="y_head")
-        product(weights0, 0, 256, y_head, 0)
-        scatter(0, 0, 256, y_head)
-        y_rest = keep.tile([P, 768], F32, name="y_rest")
-        product(weights0, 256, 512, y_rest, 256)
-        product(weights0, 512, 1024, y_rest, 256)
-
-        scatter(0, 256, 1024, y_rest)
+        y_head = keep.tile([P, HEAD], F32, name="y_head")
+        product(0, 0, HEAD, y_head, 0)
+        scatter(0, 0, HEAD, y_head)
+        y_rest = keep.tile([P, S - HEAD], F32, name="y_rest")
+        product(0, HEAD, 512, y_rest, HEAD)
+        product(0, 512, S, y_rest, HEAD)
+        scatter(0, HEAD, S, y_rest)
         nc.sync.dma_start(out[0:P, :], windows[0][:])
 
         y_second = keep.tile([P, S], F32, name="y_second")
-        product(weights1, 0, 512, y_second, 0)
-        product(weights1, 512, 1024, y_second, 0)
-        scatter(1, 0, 1024, y_second)
+        product(1, 0, 512, y_second, 0)
+        product(1, 512, S, y_second, 0)
+        scatter(1, 0, S, y_second)
         nc.sync.dma_start(out[P:2 * P, :], windows[1][:])

@@ -29,12 +29,28 @@ def tile_picked_route2_linnone_p_kernel(tc, x_words, x_scales, gate, w1, offs, d
         dst_sb = keep.tile([P, S // 16], U16, name="dst_sb")
         scales = keep.tile([P, T], U8, name="scales", tag="bytes_then_codes", align_bytes=64)
         windows = [keep.tile([P, U], F32, name=f"window{b}") for b in range(2)]
-        w_raw = keep.tile([P, PACK, N], F32, name="w_raw", tag="weights_then_gate")
+        w_rows = w1.rearrange("(p j) m -> p j m", j=PACK)
+
+        def load_weights(b):
+            raw = keep.tile([P, PACK, P], F32, name=f"w_raw{b}", tag="w_raw")
+            nc.sync.dma_start(raw[:], w_rows[:, :, b * P:(b + 1) * P])
+            return raw
+
+        def interleave_weights(b, raw):
+            grouped = keep.tile([P, P, PACK], BF16, name=f"w_grouped{b}", tag=("weights_then_gate", "w_grouped")[b], align_bytes=64)
+            nc.scalar.copy(grouped[:], raw[:].rearrange("p j m -> p m j"))
+            return grouped
+
+        def quantize_weights(b, grouped):
+            codes = keep.tile([P, P], U32, name=f"w_codes{b}", align_bytes=64)
+            plane = keep.tile([P, P], U8, name=f"w_plane{b}", align_bytes=64)
+            nc.vector.quantize_mx(out=codes[:].bitcast(FP8X4), scales=plane[:], in_=grouped[:].rearrange("p m j -> p (m j)"))
+            return codes, plane
 
         zeros = keep.tile([P, SEED], F32, name="zeros", tag="zeros_then_words", align_bytes=64)
         nc.vector.memset(zeros[:], 0.0)
         nc.vector.memset(scales[:].bitcast(I32), 0)
-        nc.sync.dma_start(w_raw[:], w1.rearrange("(p j) m -> p j m", j=PACK))
+        raw0 = load_weights(0)
         nc.sync.dma_start(offs_sb[:], offs)
         nc.sync.dma_start(dst_sb[:], dst)
         for r in range(4):
@@ -44,30 +60,31 @@ def tile_picked_route2_linnone_p_kernel(tc, x_words, x_scales, gate, w1, offs, d
         words = keep.tile([P, T], I32, name="words", tag="zeros_then_words", align_bytes=64)
         nc.sync.dma_start(words[:], x_words[0].rearrange("p c t -> p (c t)").bitcast(I32))
         nc.vector.memset(windows[0][:, SEED:U], 0.0)
-        nc.scalar.copy(windows[1][:].rearrange("p (a c) -> p a c", c=SEED), windows[0][:, 0:SEED].unsqueeze(1).to_broadcast([P, U // SEED, SEED]))
+        nc.vector.memset(windows[1][:, 0:U // 2], 0.0)
+        nc.scalar.copy(windows[1][:, U // 2:U].rearrange("p (a c) -> p a c", c=SEED), windows[0][:, 0:SEED].unsqueeze(1).to_broadcast([P, U // 2 // SEED, SEED]))
 
-        w_grouped = keep.tile([P, N, PACK], BF16, name="w_grouped", align_bytes=64)
-        nc.scalar.copy(w_grouped[:], w_raw[:].rearrange("p j m -> p m j"))
-        gate_sb = keep.tile([P, S], F32, name="gate_sb", tag="weights_then_gate")
-        nc.sync.dma_start(gate_sb[:], gate)
+        weights = [quantize_weights(0, interleave_weights(0, raw0))]
+        raw1 = load_weights(1)
+        gate_sb = keep.tile([P, S], F32, name="gate_sb", tag="weights_then_gate", align_bytes=64)
+        nc.sync.dma_start(gate_sb[:, 0:HEAD], gate[:, 0:HEAD])
+        nc.sync.dma_start(gate_sb[:, HEAD:S], gate[:, HEAD:S])
 
         x_plane = keep.tile([P, S], U8, name="x_plane", align_bytes=64)
         nc.vector.tensor_copy(x_plane[:], scales[:].indirect(offs_sb[:]))
 
-        w_codes = keep.tile([P, N], U32, name="w_codes", align_bytes=64)
-        w_plane = keep.tile([P, N], U8, name="w_plane", align_bytes=64)
-        nc.vector.quantize_mx(out=w_codes[:].bitcast(FP8X4), scales=w_plane[:], in_=w_grouped[:].rearrange("p m j -> p (m j)"))
 
         x_codes = keep.tile([P, S], U32, name="x_codes", tag="bytes_then_codes", align_bytes=64)
         for h in range(2):
             nc.vector.tensor_copy(x_codes[:, 512 * h:512 * (h + 1)], words[:].bitcast(U32).indirect(offs_sb[:, 32 * h:32 * (h + 1)]))
 
+        weights.append(quantize_weights(1, interleave_weights(1, raw1)))
+
         def product(b, lo, hi, y, y0):
             acc = psum.tile([P, hi - lo], F32, name="acc", tag="acc", bufs=5)
             nc.tensor.matmul_mx(
                 out=acc[:],
-                lhsT=w_codes[:, b * P:(b + 1) * P].bitcast(FP8X4),
-                lhsT_scale=w_plane[:, b * P:(b + 1) * P],
+                lhsT=weights[b][0][:].bitcast(FP8X4),
+                lhsT_scale=weights[b][1][:],
                 rhs=x_codes[:, lo:hi].bitcast(FP8X4),
                 rhs_scale=x_plane[:, lo:hi],
                 start=True,

@@ -48,7 +48,7 @@ def tile_picked_route2_linnone_p_kernel(tc, x_words, x_scales, gate, w1, offs, d
             return codes, plane
 
         zeros = keep.tile([P, SEED], F32, name="zeros", tag="zeros_then_words", align_bytes=64)
-        nc.vector.memset(zeros[:], 0.0)
+        nc.gpsimd.memset(zeros[:], 0.0)
         nc.vector.memset(scales[:].bitcast(I32), 0)
         raw0 = load_weights(0)
         nc.sync.dma_start(offs_sb[:], offs)
@@ -80,7 +80,7 @@ def tile_picked_route2_linnone_p_kernel(tc, x_words, x_scales, gate, w1, offs, d
         weights.append(quantize_weights(1, interleave_weights(1, raw1)))
 
         def product(b, lo, hi, y, y0):
-            acc = psum.tile([P, hi - lo], F32, name="acc", tag="acc", bufs=5)
+            acc = psum.tile([P, hi - lo], F32, name="acc", tag="acc", bufs=6)
             nc.tensor.matmul_mx(
                 out=acc[:],
                 lhsT=weights[b][0][:].bitcast(FP8X4),
@@ -95,17 +95,13 @@ def tile_picked_route2_linnone_p_kernel(tc, x_words, x_scales, gate, w1, offs, d
         def scatter(b, lo, hi, y):
             nc.vector.tensor_tensor(windows[b][:].indirect(dst_sb[:, lo // 16:hi // 16]), y[:], gate_sb[:, lo:hi], MULT)
 
-        y_head = keep.tile([P, HEAD], F32, name="y_head")
-        product(0, 0, HEAD, y_head, 0)
-        scatter(0, 0, HEAD, y_head)
-        y_rest = keep.tile([P, S - HEAD], F32, name="y_rest")
-        product(0, HEAD, 512, y_rest, HEAD)
-        product(0, 512, S, y_rest, HEAD)
-        scatter(0, HEAD, S, y_rest)
-        nc.sync.dma_start(out[0:P, :], windows[0][:])
-
-        y_second = keep.tile([P, S], F32, name="y_second")
-        product(1, 0, 512, y_second, 0)
-        product(1, 512, S, y_second, 0)
-        scatter(1, 0, S, y_second)
-        nc.sync.dma_start(out[P:2 * P, :], windows[1][:])
+        for b in range(2):
+            y_head = keep.tile([P, HEAD], F32, name=f"y_head{b}")
+            product(b, 0, HEAD, y_head, 0)
+            scatter(b, 0, HEAD, y_head)
+        for b in range(2):
+            y_rest = keep.tile([P, S - HEAD], F32, name=f"y_rest{b}")
+            product(b, HEAD, 512, y_rest, HEAD)
+            product(b, 512, S, y_rest, HEAD)
+            scatter(b, HEAD, S, y_rest)
+            nc.sync.dma_start(out[b * P:(b + 1) * P, :], windows[b][:])

@@ -80,7 +80,7 @@ def tile_picked_route2_linnone_p_kernel(tc, x_words, x_scales, gate, w1, offs, d
         weights.append(quantize_weights(1, interleave_weights(1, raw1)))
 
         def product(b, lo, hi, y, y0):
-            acc = psum.tile([P, hi - lo], F32, name="acc", tag="acc", bufs=6)
+            acc = psum.tile([P, hi - lo], F32, name="acc", tag="acc", bufs=8)
             nc.tensor.matmul_mx(
                 out=acc[:],
                 lhsT=weights[b][0][:].bitcast(FP8X4),
@@ -97,11 +97,13 @@ def tile_picked_route2_linnone_p_kernel(tc, x_words, x_scales, gate, w1, offs, d
 
         for b in range(2):
             y_head = keep.tile([P, HEAD], F32, name=f"y_head{b}")
-            product(b, 0, HEAD, y_head, 0)
+            product(b, 0, HEAD // 2, y_head, 0)
+            product(b, HEAD // 2, HEAD, y_head, 0)
             scatter(b, 0, HEAD, y_head)
         for b in range(2):
             y_rest = keep.tile([P, S - HEAD], F32, name=f"y_rest{b}")
             product(b, HEAD, 512, y_rest, HEAD)
             product(b, 512, S, y_rest, HEAD)
             scatter(b, HEAD, S, y_rest)
-            nc.sync.dma_start(out[b * P:(b + 1) * P, :], windows[b][:])
+            nc.sync.dma_start(out[b * P:(b + 1) * P, 0:U // 2], windows[b][:, 0:U // 2])
+            nc.scalar.dma_start(out[b * P:(b + 1) * P, U // 2:U], windows[b][:, U // 2:U])

@@ -27,53 +27,51 @@ def tile_picked_route2_linnone_p_kernel(tc, x_words, x_scales, gate, w1, offs, d
 
         offs_sb = keep.tile([P, S // 16], U16, name="offs_sb")
         dst_sb = keep.tile([P, S // 16], U16, name="dst_sb")
-        scales = keep.tile([P, T], U8, name="scales", tag="bytes_then_codes", align_bytes=64)
         windows = [keep.tile([P, U], F32, name=f"window{b}") for b in range(2)]
         w_rows = w1.rearrange("(p j) m -> p j m", j=PACK)
 
         def load_weights(b):
-            raw = keep.tile([P, PACK, P], F32, name=f"w_raw{b}", tag="w_raw")
+            raw = keep.tile([P, PACK, P], F32, name=f"w_raw{b}")
             nc.sync.dma_start(raw[:], w_rows[:, :, b * P:(b + 1) * P])
             return raw
 
         def interleave_weights(b, raw):
-            grouped = keep.tile([P, P, PACK], BF16, name=f"w_grouped{b}", tag=("weights_then_gate", "w_grouped")[b], align_bytes=64)
+            grouped = keep.tile([P, P, PACK], BF16, name=f"w_grouped{b}", tag=("grouped_then_codes", "picked_then_grouped")[b], align_bytes=64)
             nc.scalar.copy(grouped[:], raw[:].rearrange("p j m -> p m j"))
             return grouped
 
         def quantize_weights(b, grouped):
-            codes = keep.tile([P, P], U32, name=f"w_codes{b}", align_bytes=64)
+            codes = keep.tile([P, P], U32, name=f"w_codes{b}", tag=("scales_then_codes", "w_codes")[b], align_bytes=64)
             plane = keep.tile([P, P], U8, name=f"w_plane{b}", align_bytes=64)
             nc.vector.quantize_mx(out=codes[:].bitcast(FP8X4), scales=plane[:], in_=grouped[:].rearrange("p m j -> p (m j)"))
             return codes, plane
 
-        zeros = keep.tile([P, SEED], F32, name="zeros", tag="zeros_then_words", align_bytes=64)
-        nc.gpsimd.memset(zeros[:], 0.0)
+        scales = keep.tile([P, T], U8, name="scales", tag="scales_then_codes", align_bytes=64)
+        x_plane = keep.tile([P, S], U8, name="x_plane", align_bytes=64)
+        words = keep.tile([P, T], I32, name="words", align_bytes=64)
+        gate_sb = keep.tile([P, S], F32, name="gate_sb", align_bytes=64)
+
         nc.vector.memset(scales[:].bitcast(I32), 0)
         raw0 = load_weights(0)
         nc.sync.dma_start(offs_sb[:], offs)
         nc.sync.dma_start(dst_sb[:], dst)
-        for r in range(4):
-            nc.sync.dma_start(scales[r:P:32, :].bitcast(I32), x_scales[0, r:16:4, :].bitcast(I32))
-
-        nc.vector.tensor_copy(windows[0][:, 0:SEED], zeros[:])
-        words = keep.tile([P, T], I32, name="words", tag="zeros_then_words", align_bytes=64)
         nc.sync.dma_start(words[:], x_words[0].rearrange("p c t -> p (c t)").bitcast(I32))
-        nc.vector.memset(windows[0][:, SEED:U], 0.0)
-        nc.vector.memset(windows[1][:, 0:U // 2], 0.0)
-        nc.scalar.copy(windows[1][:, U // 2:U].rearrange("p (a c) -> p a c", c=SEED), windows[0][:, 0:SEED].unsqueeze(1).to_broadcast([P, U // 2 // SEED, SEED]))
-
-        weights = [quantize_weights(0, interleave_weights(0, raw0))]
+        nc.scalar.dma_start(scales[0:P:8, :].bitcast(I32), x_scales[0].bitcast(I32))
         raw1 = load_weights(1)
-        gate_sb = keep.tile([P, S], F32, name="gate_sb", tag="weights_then_gate", align_bytes=64)
-        nc.sync.dma_start(gate_sb[:, 0:HEAD], gate[:, 0:HEAD])
-        nc.sync.dma_start(gate_sb[:, HEAD:S], gate[:, HEAD:S])
+        nc.sync.dma_start(gate_sb[:], gate)
 
-        x_plane = keep.tile([P, S], U8, name="x_plane", align_bytes=64)
-        nc.vector.tensor_copy(x_plane[:], scales[:].indirect(offs_sb[:]))
+        nc.vector.memset(x_plane[:].bitcast(I32), 0)
+        nc.vector.memset(windows[0][:], 0.0)
+        grouped0 = interleave_weights(0, raw0)
+        nc.scalar.copy(windows[1][:].rearrange("p (a c) -> p a c", c=SEED), windows[0][:, 0:SEED].unsqueeze(1).to_broadcast([P, U // SEED, SEED]))
 
+        picked = keep.tile([P, S], U8, name="picked", tag="picked_then_grouped", align_bytes=64)
+        nc.vector.tensor_copy(picked[:], scales[:].indirect(offs_sb[:]))
+        for r in range(4):
+            nc.scalar.dma_start(x_plane[r:P:32, :].bitcast(I32), picked[8 * r:P:32, :].bitcast(I32))
+        weights = [quantize_weights(0, grouped0)]
 
-        x_codes = keep.tile([P, S], U32, name="x_codes", tag="bytes_then_codes", align_bytes=64)
+        x_codes = keep.tile([P, S], U32, name="x_codes", tag="grouped_then_codes", align_bytes=64)
         for h in range(2):
             nc.vector.tensor_copy(x_codes[:, 512 * h:512 * (h + 1)], words[:].bitcast(U32).indirect(offs_sb[:, 32 * h:32 * (h + 1)]))
 

@@ -31,47 +31,50 @@ def tile_picked_route2_linnone_p_kernel(tc, x_words, x_scales, gate, w1, offs, d
         w_rows = w1.rearrange("(p j) m -> p j m", j=PACK)
 
         def load_weights(b):
-            raw = keep.tile([P, PACK, P], F32, name=f"w_raw{b}")
+            raw = keep.tile([P, PACK, P], F32, name=f"w_raw{b}", tag=("w_raw", "scales_then_raw")[b], align_bytes=64)
             nc.sync.dma_start(raw[:], w_rows[:, :, b * P:(b + 1) * P])
             return raw
 
         def interleave_weights(b, raw):
-            grouped = keep.tile([P, P, PACK], BF16, name=f"w_grouped{b}", tag=("grouped_then_codes", "picked_then_grouped")[b], align_bytes=64)
+            grouped = keep.tile([P, P, PACK], BF16, name=f"w_grouped{b}", tag=("grouped_then_gate", "w_grouped")[b], align_bytes=64)
             nc.scalar.copy(grouped[:], raw[:].rearrange("p j m -> p m j"))
             return grouped
 
         def quantize_weights(b, grouped):
-            codes = keep.tile([P, P], U32, name=f"w_codes{b}", tag=("scales_then_codes", "w_codes")[b], align_bytes=64)
+            codes = keep.tile([P, P], U32, name=f"w_codes{b}", align_bytes=64)
             plane = keep.tile([P, P], U8, name=f"w_plane{b}", align_bytes=64)
             nc.vector.quantize_mx(out=codes[:].bitcast(FP8X4), scales=plane[:], in_=grouped[:].rearrange("p m j -> p (m j)"))
             return codes, plane
 
-        scales = keep.tile([P, T], U8, name="scales", tag="scales_then_codes", align_bytes=64)
+        scales = keep.tile([P, T], U8, name="scales", tag="scales_then_raw", align_bytes=64)
         x_plane = keep.tile([P, S], U8, name="x_plane", align_bytes=64)
         words = keep.tile([P, T], I32, name="words", align_bytes=64)
-        gate_sb = keep.tile([P, S], F32, name="gate_sb", align_bytes=64)
 
-        nc.vector.memset(scales[:].bitcast(I32), 0)
         raw0 = load_weights(0)
+        nc.sync.dma_start(scales[P - 16:P, :].bitcast(I32), x_scales[0].bitcast(I32))
         nc.sync.dma_start(offs_sb[:], offs)
         nc.sync.dma_start(dst_sb[:], dst)
         nc.sync.dma_start(words[:], x_words[0].rearrange("p c t -> p (c t)").bitcast(I32))
-        nc.scalar.dma_start(scales[0:P:8, :].bitcast(I32), x_scales[0].bitcast(I32))
-        raw1 = load_weights(1)
-        nc.sync.dma_start(gate_sb[:], gate)
 
+        nc.vector.memset(scales[0:P - 16, :].bitcast(I32), 0)
         nc.vector.memset(x_plane[:].bitcast(I32), 0)
-        nc.vector.memset(windows[0][:], 0.0)
+        zeros = keep.tile([P, SEED], F32, name="zeros")
+        nc.gpsimd.memset(zeros[:], 0.0)
         grouped0 = interleave_weights(0, raw0)
-        nc.scalar.copy(windows[1][:].rearrange("p (a c) -> p a c", c=SEED), windows[0][:, 0:SEED].unsqueeze(1).to_broadcast([P, U // SEED, SEED]))
+        for b in range(2):
+            nc.scalar.copy(windows[b][:].rearrange("p (a c) -> p a c", c=SEED), zeros[:].unsqueeze(1).to_broadcast([P, U // SEED, SEED]))
 
-        picked = keep.tile([P, S], U8, name="picked", tag="picked_then_grouped", align_bytes=64)
+        picked = keep.tile([P, S], U8, name="picked", align_bytes=64)
         nc.vector.tensor_copy(picked[:], scales[:].indirect(offs_sb[:]))
-        for r in range(4):
-            nc.scalar.dma_start(x_plane[r:P:32, :].bitcast(I32), picked[8 * r:P:32, :].bitcast(I32))
+        for q in range(4):
+            nc.sync.dma_start(x_plane[32 * q:32 * q + 4, :].bitcast(I32), picked[P - 16 + 4 * q:P - 12 + 4 * q, :].bitcast(I32))
         weights = [quantize_weights(0, grouped0)]
+        raw1 = load_weights(1)
+        gate_sb = keep.tile([P, S], F32, name="gate_sb", tag="grouped_then_gate", align_bytes=64)
+        nc.sync.dma_start(gate_sb[:, 0:HEAD], gate[:, 0:HEAD])
+        nc.sync.dma_start(gate_sb[:, HEAD:S], gate[:, HEAD:S])
 
-        x_codes = keep.tile([P, S], U32, name="x_codes", tag="grouped_then_codes", align_bytes=64)
+        x_codes = keep.tile([P, S], U32, name="x_codes", align_bytes=64)
         for h in range(2):
             nc.vector.tensor_copy(x_codes[:, 512 * h:512 * (h + 1)], words[:].bitcast(U32).indirect(offs_sb[:, 32 * h:32 * (h + 1)]))
 
@@ -94,7 +97,7 @@ def tile_picked_route2_linnone_p_kernel(tc, x_words, x_scales, gate, w1, offs, d
             nc.vector.tensor_tensor(windows[b][:].indirect(dst_sb[:, lo // 16:hi // 16]), y[:], gate_sb[:, lo:hi], MULT)
 
         for b in range(2):
-            y_head = keep.tile([P, HEAD], F32, name=f"y_head{b}")
+            y_head = keep.tile([P, HEAD], F32, name=f"y_head{b}", tag=("scales_then_raw", "y_head")[b], align_bytes=64)
             product(b, 0, HEAD // 2, y_head, 0)
             product(b, HEAD // 2, HEAD, y_head, 0)
             scatter(b, 0, HEAD, y_head)

@@ -48,26 +48,27 @@ def tile_picked_route2_linnone_p_kernel(tc, x_words, x_scales, gate, w1, offs, d
 
         scales = keep.tile([P, T], U8, name="scales", tag="scales_then_raw", align_bytes=64)
         x_plane = keep.tile([P, S], U8, name="x_plane", align_bytes=64)
-        words = keep.tile([P, T], I32, name="words", align_bytes=64)
 
+        zeros = keep.tile([P, SEED], F32, name="zeros", tag="zeros_then_words", align_bytes=64)
+        nc.gpsimd.memset(zeros[:], 0.0)
+        nc.vector.memset(scales[:].bitcast(I32), 0)
         raw0 = load_weights(0)
-        nc.sync.dma_start(scales[P - 16:P, :].bitcast(I32), x_scales[0].bitcast(I32))
         nc.sync.dma_start(offs_sb[:], offs)
         nc.sync.dma_start(dst_sb[:], dst)
+        nc.sync.dma_start(scales[11:11 + 7 * 15 + 1:7, :].bitcast(I32), x_scales[0].bitcast(I32))
+        nc.vector.tensor_copy(windows[0][:, 0:SEED], zeros[:])
+        words = keep.tile([P, T], I32, name="words", tag="zeros_then_words", align_bytes=64)
         nc.sync.dma_start(words[:], x_words[0].rearrange("p c t -> p (c t)").bitcast(I32))
 
-        nc.vector.memset(scales[0:P - 16, :].bitcast(I32), 0)
         nc.vector.memset(x_plane[:].bitcast(I32), 0)
-        zeros = keep.tile([P, SEED], F32, name="zeros")
-        nc.gpsimd.memset(zeros[:], 0.0)
         grouped0 = interleave_weights(0, raw0)
-        for b in range(2):
-            nc.scalar.copy(windows[b][:].rearrange("p (a c) -> p a c", c=SEED), zeros[:].unsqueeze(1).to_broadcast([P, U // SEED, SEED]))
+        nc.scalar.copy(windows[0][:, SEED:U].rearrange("p (a c) -> p a c", c=SEED), windows[0][:, 0:SEED].unsqueeze(1).to_broadcast([P, U // SEED - 1, SEED]))
+        nc.scalar.copy(windows[1][:].rearrange("p (a c) -> p a c", c=SEED), windows[0][:, 0:SEED].unsqueeze(1).to_broadcast([P, U // SEED, SEED]))
 
         picked = keep.tile([P, S], U8, name="picked", align_bytes=64)
         nc.vector.tensor_copy(picked[:], scales[:].indirect(offs_sb[:]))
-        for q in range(4):
-            nc.sync.dma_start(x_plane[32 * q:32 * q + 4, :].bitcast(I32), picked[P - 16 + 4 * q:P - 12 + 4 * q, :].bitcast(I32))
+        for r in range(4):
+            nc.sync.dma_start(x_plane[r:P:32, :].bitcast(I32), picked[11 + 7 * r:11 + 7 * r + 28 * 3 + 1:28, :].bitcast(I32))
         weights = [quantize_weights(0, grouped0)]
         raw1 = load_weights(1)
         gate_sb = keep.tile([P, S], F32, name="gate_sb", tag="grouped_then_gate", align_bytes=64)

@@ -50,7 +50,7 @@ def tile_picked_route2_linnone_p_kernel(tc, x_words, x_scales, gate, w1, offs, d
         x_plane = keep.tile([P, S], U8, name="x_plane", align_bytes=64)
 
         zeros = keep.tile([P, SEED], F32, name="zeros", tag="zeros_then_words", align_bytes=64)
-        nc.gpsimd.memset(zeros[:], 0.0)
+        nc.vector.memset(zeros[:], 0.0)
         nc.vector.memset(scales[:].bitcast(I32), 0)
         raw0 = load_weights(0)
         nc.sync.dma_start(offs_sb[:], offs)
@@ -107,5 +107,4 @@ def tile_picked_route2_linnone_p_kernel(tc, x_words, x_scales, gate, w1, offs, d
             product(b, HEAD, 512, y_rest, HEAD)
             product(b, 512, S, y_rest, HEAD)
             scatter(b, HEAD, S, y_rest)
-            nc.sync.dma_start(out[b * P:(b + 1) * P, 0:U // 2], windows[b][:, 0:U // 2])
-            nc.scalar.dma_start(out[b * P:(b + 1) * P, U // 2:U], windows[b][:, U // 2:U])
+            nc.sync.dma_start(out[b * P:(b + 1) * P, :], windows[b][:])

@@ -6,7 +6,7 @@ K, T, S, N, U = 512, 4096, 1024, 256, 2048
 P = 128
 PACK = 4
 FLOPS = 2 * K * N * S
-HEAD = 256
+HEAD = 384
 SEED = 64
 
 F32 = mybir.dt.float32
@@ -23,6 +23,7 @@ def tile_picked_route2_linnone_p_kernel(tc, x_words, x_scales, gate, w1, offs, d
     nc = tc.nc
     with ExitStack() as ctx:
         keep = ctx.enter_context(tc.tile_pool(name="keep", bufs=1))
+        reuse = ctx.enter_context(tc.tile_pool(name="reuse", bufs=1))
         psum = ctx.enter_context(tc.psum_pool(name="psum", bufs=1))
 
         offs_sb = keep.tile([P, S // 16], U16, name="offs_sb")
@@ -30,13 +31,12 @@ def tile_picked_route2_linnone_p_kernel(tc, x_words, x_scales, gate, w1, offs, d
         windows = [keep.tile([P, U], F32, name=f"window{b}") for b in range(2)]
         w_rows = w1.rearrange("(p j) m -> p j m", j=PACK)
 
-        def load_weights(b):
-            raw = keep.tile([P, PACK, P], F32, name=f"w_raw{b}", tag=("w_raw", "scales_then_raw")[b], align_bytes=64)
+        def load_weights(b, raw):
             nc.sync.dma_start(raw[:], w_rows[:, :, b * P:(b + 1) * P])
             return raw
 
         def interleave_weights(b, raw):
-            grouped = keep.tile([P, P, PACK], BF16, name=f"w_grouped{b}", tag=("grouped_then_gate", "w_grouped")[b], align_bytes=64)
+            grouped = keep.tile([P, P, PACK], BF16, name=f"w_grouped{b}", align_bytes=64)
             nc.scalar.copy(grouped[:], raw[:].rearrange("p j m -> p m j"))
             return grouped
 
@@ -46,19 +46,20 @@ def tile_picked_route2_linnone_p_kernel(tc, x_words, x_scales, gate, w1, offs, d
             nc.vector.quantize_mx(out=codes[:].bitcast(FP8X4), scales=plane[:], in_=grouped[:].rearrange("p m j -> p (m j)"))
             return codes, plane
 
-        scales = keep.tile([P, T], U8, name="scales", tag="scales_then_raw", align_bytes=64)
+        scales = keep.tile([P, T], U8, name="scales", tag="scales_then_gate", align_bytes=64)
         x_plane = keep.tile([P, S], U8, name="x_plane", align_bytes=64)
 
-        zeros = keep.tile([P, SEED], F32, name="zeros", tag="zeros_then_words", align_bytes=64)
+        zeros = reuse.tile([P, SEED], F32, name="zeros", offset=4 * T - 128, align_bytes=64)
         nc.vector.memset(zeros[:], 0.0)
         nc.vector.memset(scales[:].bitcast(I32), 0)
-        raw0 = load_weights(0)
+        raw0 = load_weights(0, keep.tile([P, PACK, P], F32, name="w_raw0"))
         nc.sync.dma_start(offs_sb[:], offs)
         nc.sync.dma_start(dst_sb[:], dst)
         nc.sync.dma_start(scales[11:11 + 7 * 15 + 1:7, :].bitcast(I32), x_scales[0].bitcast(I32))
         nc.vector.tensor_copy(windows[0][:, 0:SEED], zeros[:])
-        words = keep.tile([P, T], I32, name="words", tag="zeros_then_words", align_bytes=64)
+        words = reuse.tile([P, T], I32, name="words", offset=0, align_bytes=64)
         nc.sync.dma_start(words[:], x_words[0].rearrange("p c t -> p (c t)").bitcast(I32))
+        raw1 = load_weights(1, reuse.tile([P, PACK, P], F32, name="w_raw1", offset=4 * T, align_bytes=64))
 
         nc.vector.memset(x_plane[:].bitcast(I32), 0)
         grouped0 = interleave_weights(0, raw0)
@@ -70,8 +71,7 @@ def tile_picked_route2_linnone_p_kernel(tc, x_words, x_scales, gate, w1, offs, d
         for r in range(4):
             nc.sync.dma_start(x_plane[r:P:32, :].bitcast(I32), picked[11 + 7 * r:11 + 7 * r + 28 * 3 + 1:28, :].bitcast(I32))
         weights = [quantize_weights(0, grouped0)]
-        raw1 = load_weights(1)
-        gate_sb = keep.tile([P, S], F32, name="gate_sb", tag="grouped_then_gate", align_bytes=64)
+        gate_sb = keep.tile([P, S], F32, name="gate_sb", tag="scales_then_gate", align_bytes=64)
         nc.sync.dma_start(gate_sb[:, 0:HEAD], gate[:, 0:HEAD])
         nc.sync.dma_start(gate_sb[:, HEAD:S], gate[:, HEAD:S])
 
@@ -97,14 +97,20 @@ def tile_picked_route2_linnone_p_kernel(tc, x_words, x_scales, gate, w1, offs, d
         def scatter(b, lo, hi, y):
             nc.vector.tensor_tensor(windows[b][:].indirect(dst_sb[:, lo // 16:hi // 16]), y[:], gate_sb[:, lo:hi], MULT)
 
-        for b in range(2):
-            y_head = keep.tile([P, HEAD], F32, name=f"y_head{b}", tag=("scales_then_raw", "y_head")[b], align_bytes=64)
-            product(b, 0, HEAD // 2, y_head, 0)
-            product(b, HEAD // 2, HEAD, y_head, 0)
-            scatter(b, 0, HEAD, y_head)
-        for b in range(2):
-            y_rest = keep.tile([P, S - HEAD], F32, name=f"y_rest{b}")
-            product(b, HEAD, 512, y_rest, HEAD)
-            product(b, 512, S, y_rest, HEAD)
-            scatter(b, HEAD, S, y_rest)
+        def store(b):
             nc.sync.dma_start(out[b * P:(b + 1) * P, :], windows[b][:])
+
+        y_head = reuse.tile([P, HEAD], F32, name="y_head", offset=4 * T, align_bytes=64)
+        for lo in range(0, HEAD, P):
+            product(0, lo, lo + P, y_head, 0)
+        scatter(0, 0, HEAD, y_head)
+        y_all = keep.tile([P, S], F32, name="y_all")
+        product(1, 0, 512, y_all, 0)
+        product(1, 512, S, y_all, 0)
+        scatter(1, 0, S, y_all)
+        store(1)
+        y_rest = keep.tile([P, S - HEAD], F32, name="y_rest")
+        product(0, HEAD, 512, y_rest, HEAD)
+        product(0, 512, S, y_rest, HEAD)
+        scatter(0, HEAD, S, y_rest)
+        store(0)

@@ -62,8 +62,8 @@ def tile_picked_route2_linnone_p_kernel(tc, x_words, x_scales, gate, w1, offs, d
         raw1 = load_weights(1, reuse.tile([P, PACK, P], F32, name="w_raw1", offset=4 * T, align_bytes=64))
 
         nc.vector.memset(x_plane[:].bitcast(I32), 0)
+        nc.vector.memset(windows[0][:, SEED:U], 0.0)
         grouped0 = interleave_weights(0, raw0)
-        nc.scalar.copy(windows[0][:, SEED:U].rearrange("p (a c) -> p a c", c=SEED), windows[0][:, 0:SEED].unsqueeze(1).to_broadcast([P, U // SEED - 1, SEED]))
         nc.scalar.copy(windows[1][:].rearrange("p (a c) -> p a c", c=SEED), windows[0][:, 0:SEED].unsqueeze(1).to_broadcast([P, U // SEED, SEED]))
 
         picked = keep.tile([P, S], U8, name="picked", align_bytes=64)

@@ -8,6 +8,7 @@ PACK = 4
 FLOPS = 2 * K * N * S
 HEAD = 384
 SEED = 64
+SECOND = 4 * T + 2048
 
 F32 = mybir.dt.float32
 BF16 = mybir.dt.bfloat16
@@ -31,19 +32,19 @@ def tile_picked_route2_linnone_p_kernel(tc, x_words, x_scales, gate, w1, offs, d
         windows = [keep.tile([P, U], F32, name=f"window{b}") for b in range(2)]
         w_rows = w1.rearrange("(p j) m -> p j m", j=PACK)
 
-        def load_weights(b, raw):
-            nc.sync.dma_start(raw[:], w_rows[:, :, b * P:(b + 1) * P])
+        grouped = [keep.tile([P, P, PACK], BF16, name=f"w_grouped{b}", align_bytes=64) for b in range(2)]
+
+        def load_weights(j, m0, m1, raw):
+            nc.sync.dma_start(raw[:], w_rows[:, j:j + 2, m0:m1])
             return raw
 
-        def interleave_weights(b, raw):
-            grouped = keep.tile([P, P, PACK], BF16, name=f"w_grouped{b}", align_bytes=64)
-            nc.scalar.copy(grouped[:], raw[:].rearrange("p j m -> p m j"))
-            return grouped
+        def interleave_weights(b, j, raw):
+            nc.scalar.copy(grouped[b][:, :, j:j + 2], raw.rearrange("p j m -> p m j"))
 
-        def quantize_weights(b, grouped):
+        def quantize_weights(b):
             codes = keep.tile([P, P], U32, name=f"w_codes{b}", align_bytes=64)
             plane = keep.tile([P, P], U8, name=f"w_plane{b}", align_bytes=64)
-            nc.vector.quantize_mx(out=codes[:].bitcast(FP8X4), scales=plane[:], in_=grouped[:].rearrange("p m j -> p (m j)"))
+            nc.vector.quantize_mx(out=codes[:].bitcast(FP8X4), scales=plane[:], in_=grouped[b][:].rearrange("p m j -> p (m j)"))
             return codes, plane
 
         scales = keep.tile([P, T], U8, name="scales", tag="scales_then_gate", align_bytes=64)
@@ -52,34 +53,40 @@ def tile_picked_route2_linnone_p_kernel(tc, x_words, x_scales, gate, w1, offs, d
         zeros = reuse.tile([P, SEED], F32, name="zeros", offset=4 * T - 128, align_bytes=64)
         nc.vector.memset(zeros[:], 0.0)
         nc.vector.memset(scales[:].bitcast(I32), 0)
-        raw0 = load_weights(0, keep.tile([P, PACK, P], F32, name="w_raw0"))
+        front = load_weights(0, 0, N, reuse.tile([P, 2, N], F32, name="w_front", offset=SECOND, align_bytes=64))
         nc.sync.dma_start(offs_sb[:], offs)
         nc.sync.dma_start(dst_sb[:], dst)
         nc.sync.dma_start(scales[11:11 + 7 * 15 + 1:7, :].bitcast(I32), x_scales[0].bitcast(I32))
         nc.vector.tensor_copy(windows[0][:, 0:SEED], zeros[:])
         words = reuse.tile([P, T], I32, name="words", offset=0, align_bytes=64)
         nc.sync.dma_start(words[:], x_words[0].rearrange("p c t -> p (c t)").bitcast(I32))
-        raw1 = load_weights(1, reuse.tile([P, PACK, P], F32, name="w_raw1", offset=4 * T, align_bytes=64))
+        back0 = load_weights(2, 0, P, reuse.tile([P, 2, P], F32, name="w_back0", offset=4 * T, align_bytes=64))
 
         nc.vector.memset(x_plane[:].bitcast(I32), 0)
         nc.vector.memset(windows[0][:, SEED:U], 0.0)
-        grouped0 = interleave_weights(0, raw0)
+        for b in range(2):
+            interleave_weights(b, 0, front[:, :, b * P:(b + 1) * P])
+        back1 = load_weights(2, P, N, reuse.tile([P, 2, P], F32, name="w_back1", offset=SECOND, align_bytes=64))
         nc.scalar.copy(windows[1][:].rearrange("p (a c) -> p a c", c=SEED), windows[0][:, 0:SEED].unsqueeze(1).to_broadcast([P, U // SEED, SEED]))
 
         picked = keep.tile([P, S], U8, name="picked", align_bytes=64)
         nc.vector.tensor_copy(picked[:], scales[:].indirect(offs_sb[:]))
         for r in range(4):
             nc.sync.dma_start(x_plane[r:P:32, :].bitcast(I32), picked[11 + 7 * r:11 + 7 * r + 28 * 3 + 1:28, :].bitcast(I32))
-        weights = [quantize_weights(0, grouped0)]
         gate_sb = keep.tile([P, S], F32, name="gate_sb", tag="scales_then_gate", align_bytes=64)
         nc.sync.dma_start(gate_sb[:, 0:HEAD], gate[:, 0:HEAD])
         nc.sync.dma_start(gate_sb[:, HEAD:S], gate[:, HEAD:S])
 
-        x_codes = keep.tile([P, S], U32, name="x_codes", align_bytes=64)
-        for h in range(2):
-            nc.vector.tensor_copy(x_codes[:, 512 * h:512 * (h + 1)], words[:].bitcast(U32).indirect(offs_sb[:, 32 * h:32 * (h + 1)]))
+        def gather_words(h, codes):
+            nc.vector.tensor_copy(codes[:], words[:].bitcast(U32).indirect(offs_sb[:, 32 * h:32 * (h + 1)]))
+            return codes
 
-        weights.append(quantize_weights(1, interleave_weights(1, raw1)))
+        x_codes = [gather_words(0, keep.tile([P, 512], U32, name="x_codes0", align_bytes=64))]
+        interleave_weights(0, 2, back0[:])
+        weights = [quantize_weights(0)]
+        x_codes.append(gather_words(1, reuse.tile([P, 512], U32, name="x_codes1", offset=4 * T, align_bytes=64)))
+        interleave_weights(1, 2, back1[:])
+        weights.append(quantize_weights(1))
 
         def product(b, lo, hi, y, y0):
             acc = psum.tile([P, hi - lo], F32, name="acc", tag="acc", bufs=8)
@@ -87,7 +94,7 @@ def tile_picked_route2_linnone_p_kernel(tc, x_words, x_scales, gate, w1, offs, d
                 out=acc[:],
                 lhsT=weights[b][0][:].bitcast(FP8X4),
                 lhsT_scale=weights[b][1][:],
-                rhs=x_codes[:, lo:hi].bitcast(FP8X4),
+                rhs=x_codes[lo // 512][:, lo % 512:lo % 512 + hi - lo].bitcast(FP8X4),
                 rhs_scale=x_plane[:, lo:hi],
                 start=True,
                 stop=True,
@@ -100,7 +107,7 @@ def tile_picked_route2_linnone_p_kernel(tc, x_words, x_scales, gate, w1, offs, d
         def store(b):
             nc.sync.dma_start(out[b * P:(b + 1) * P, :], windows[b][:])
 
-        y_head = reuse.tile([P, HEAD], F32, name="y_head", offset=4 * T, align_bytes=64)
+        y_head = reuse.tile([P, HEAD], F32, name="y_head", offset=SECOND, align_bytes=64)
         for lo in range(0, HEAD, P):
             product(0, lo, lo + P, y_head, 0)
         scatter(0, 0, HEAD, y_head)

@@ -8,6 +8,7 @@ PACK = 4
 FLOPS = 2 * K * N * S
 HEAD = 384
 SEED = 64
+SPLIT = 3072
 SECOND = 4 * T + 2048
 
 F32 = mybir.dt.float32
@@ -34,12 +35,12 @@ def tile_picked_route2_linnone_p_kernel(tc, x_words, x_scales, gate, w1, offs, d
 
         grouped = [keep.tile([P, P, PACK], BF16, name=f"w_grouped{b}", align_bytes=64) for b in range(2)]
 
-        def load_weights(j, m0, m1, raw):
-            nc.sync.dma_start(raw[:], w_rows[:, j:j + 2, m0:m1])
+        def load_weights(b, j, raw):
+            nc.sync.dma_start(raw[:], w_rows[:, j:PACK, b * P:(b + 1) * P])
             return raw
 
-        def interleave_weights(b, j, raw):
-            nc.scalar.copy(grouped[b][:, :, j:j + 2], raw.rearrange("p j m -> p m j"))
+        def interleave_weights(b, j0, j1, raw):
+            nc.scalar.copy(grouped[b][:, :, j0:j1], raw.rearrange("p j m -> p m j"))
 
         def quantize_weights(b):
             codes = keep.tile([P, P], U32, name=f"w_codes{b}", align_bytes=64)
@@ -51,22 +52,24 @@ def tile_picked_route2_linnone_p_kernel(tc, x_words, x_scales, gate, w1, offs, d
         x_plane = keep.tile([P, S], U8, name="x_plane", align_bytes=64)
 
         zeros = reuse.tile([P, SEED], F32, name="zeros", offset=4 * T - 128, align_bytes=64)
-        nc.vector.memset(zeros[:], 0.0)
-        nc.vector.memset(scales[:].bitcast(I32), 0)
-        front = load_weights(0, 0, N, reuse.tile([P, 2, N], F32, name="w_front", offset=SECOND, align_bytes=64))
+        nc.vector.memset(scales[:, 0:SPLIT].bitcast(I32), 0)
+        nc.gpsimd.memset(scales[:, SPLIT:T].bitcast(I32), 0)
+        nc.gpsimd.memset(zeros[:], 0.0)
+        front = reuse.tile([P, 3, P], F32, name="w_front", offset=SECOND, align_bytes=64)
+        nc.sync.dma_start(front[:].rearrange("p a m -> p (a m)"), w_rows.rearrange("p j m -> p (j m)")[:, 0:3 * P])
         nc.sync.dma_start(offs_sb[:], offs)
         nc.sync.dma_start(dst_sb[:], dst)
         nc.sync.dma_start(scales[11:11 + 7 * 15 + 1:7, :].bitcast(I32), x_scales[0].bitcast(I32))
         nc.vector.tensor_copy(windows[0][:, 0:SEED], zeros[:])
         words = reuse.tile([P, T], I32, name="words", offset=0, align_bytes=64)
         nc.sync.dma_start(words[:], x_words[0].rearrange("p c t -> p (c t)").bitcast(I32))
-        back0 = load_weights(2, 0, P, reuse.tile([P, 2, P], F32, name="w_back0", offset=4 * T, align_bytes=64))
+        back0 = load_weights(0, 2, reuse.tile([P, 2, P], F32, name="w_back0", offset=4 * T, align_bytes=64))
 
         nc.vector.memset(x_plane[:].bitcast(I32), 0)
         nc.vector.memset(windows[0][:, SEED:U], 0.0)
-        for b in range(2):
-            interleave_weights(b, 0, front[:, :, b * P:(b + 1) * P])
-        back1 = load_weights(2, P, N, reuse.tile([P, 2, P], F32, name="w_back1", offset=SECOND, align_bytes=64))
+        interleave_weights(0, 0, 2, front[:, 0:3:2, :])
+        interleave_weights(1, 0, 1, front[:, 1:2, :])
+        back1 = load_weights(1, 1, reuse.tile([P, 3, P], F32, name="w_back1", offset=SECOND, align_bytes=64))
         nc.scalar.copy(windows[1][:].rearrange("p (a c) -> p a c", c=SEED), windows[0][:, 0:SEED].unsqueeze(1).to_broadcast([P, U // SEED, SEED]))
 
         picked = keep.tile([P, S], U8, name="picked", align_bytes=64)
@@ -82,10 +85,10 @@ def tile_picked_route2_linnone_p_kernel(tc, x_words, x_scales, gate, w1, offs, d
             return codes
 
         x_codes = [gather_words(0, keep.tile([P, 512], U32, name="x_codes0", align_bytes=64))]
-        interleave_weights(0, 2, back0[:])
+        interleave_weights(0, 2, PACK, back0[:])
         weights = [quantize_weights(0)]
         x_codes.append(gather_words(1, reuse.tile([P, 512], U32, name="x_codes1", offset=4 * T, align_bytes=64)))
-        interleave_weights(1, 2, back1[:])
+        interleave_weights(1, 1, PACK, back1[:])
         weights.append(quantize_weights(1))
 
         def product(b, lo, hi, y, y0):

@@ -8,7 +8,7 @@ PACK = 4
 FLOPS = 2 * K * N * S
 HEAD = 384
 SEED = 64
-SPLIT = 3072
+ROW0 = 112
 SECOND = 4 * T + 2048
 
 F32 = mybir.dt.float32
@@ -51,31 +51,28 @@ def tile_picked_route2_linnone_p_kernel(tc, x_words, x_scales, gate, w1, offs, d
         scales = keep.tile([P, T], U8, name="scales", tag="scales_then_gate", align_bytes=64)
         x_plane = keep.tile([P, S], U8, name="x_plane", align_bytes=64)
 
-        zeros = reuse.tile([P, SEED], F32, name="zeros", offset=4 * T - 128, align_bytes=64)
-        nc.vector.memset(scales[:, 0:SPLIT].bitcast(I32), 0)
-        nc.gpsimd.memset(scales[:, SPLIT:T].bitcast(I32), 0)
-        nc.gpsimd.memset(zeros[:], 0.0)
-        front = reuse.tile([P, 3, P], F32, name="w_front", offset=SECOND, align_bytes=64)
-        nc.sync.dma_start(front[:].rearrange("p a m -> p (a m)"), w_rows.rearrange("p j m -> p (j m)")[:, 0:3 * P])
+        nc.vector.memset(windows[0][:, 0:SEED], 0.0)
+        nc.vector.memset(scales[0:ROW0, :].bitcast(I32), 0)
+        nc.sync.dma_start(scales[ROW0:P, :].bitcast(I32), x_scales[0].bitcast(I32))
         nc.sync.dma_start(offs_sb[:], offs)
-        nc.sync.dma_start(dst_sb[:], dst)
-        nc.sync.dma_start(scales[11:11 + 7 * 15 + 1:7, :].bitcast(I32), x_scales[0].bitcast(I32))
-        nc.vector.tensor_copy(windows[0][:, 0:SEED], zeros[:])
+        front = keep.tile([P, 3, P], F32, name="w_front", align_bytes=64)
+        nc.sync.dma_start(front[:].rearrange("p a m -> p (a m)"), w_rows.rearrange("p j m -> p (j m)")[:, 0:3 * P])
         words = reuse.tile([P, T], I32, name="words", offset=0, align_bytes=64)
         nc.sync.dma_start(words[:], x_words[0].rearrange("p c t -> p (c t)").bitcast(I32))
         back0 = load_weights(0, 2, reuse.tile([P, 2, P], F32, name="w_back0", offset=4 * T, align_bytes=64))
+        back1 = load_weights(1, 1, reuse.tile([P, 3, P], F32, name="w_back1", offset=SECOND, align_bytes=64))
+        nc.sync.dma_start(dst_sb[:], dst)
 
         nc.vector.memset(x_plane[:].bitcast(I32), 0)
         nc.vector.memset(windows[0][:, SEED:U], 0.0)
         interleave_weights(0, 0, 2, front[:, 0:3:2, :])
         interleave_weights(1, 0, 1, front[:, 1:2, :])
-        back1 = load_weights(1, 1, reuse.tile([P, 3, P], F32, name="w_back1", offset=SECOND, align_bytes=64))
         nc.scalar.copy(windows[1][:].rearrange("p (a c) -> p a c", c=SEED), windows[0][:, 0:SEED].unsqueeze(1).to_broadcast([P, U // SEED, SEED]))
 
         picked = keep.tile([P, S], U8, name="picked", align_bytes=64)
         nc.vector.tensor_copy(picked[:], scales[:].indirect(offs_sb[:]))
         for r in range(4):
-            nc.sync.dma_start(x_plane[r:P:32, :].bitcast(I32), picked[11 + 7 * r:11 + 7 * r + 28 * 3 + 1:28, :].bitcast(I32))
+            nc.sync.dma_start(x_plane[r:P:32, :].bitcast(I32), picked[ROW0 + r:P:4, :].bitcast(I32))
         gate_sb = keep.tile([P, S], F32, name="gate_sb", tag="scales_then_gate", align_bytes=64)
         nc.sync.dma_start(gate_sb[:, 0:HEAD], gate[:, 0:HEAD])
         nc.sync.dma_start(gate_sb[:, HEAD:S], gate[:, HEAD:S])

@@ -6,7 +6,7 @@ K, T, S, N, U = 512, 4096, 1024, 256, 2048
 P = 128
 PACK = 4
 FLOPS = 2 * K * N * S
-HEAD = 384
+HEAD = 256
 SEED = 64
 ROW0 = 112
 SECOND = 4 * T + 2048
@@ -107,17 +107,14 @@ def tile_picked_route2_linnone_p_kernel(tc, x_words, x_scales, gate, w1, offs, d
         def store(b):
             nc.sync.dma_start(out[b * P:(b + 1) * P, :], windows[b][:])
 
-        y_head = reuse.tile([P, HEAD], F32, name="y_head", offset=SECOND, align_bytes=64)
-        for lo in range(0, HEAD, P):
-            product(0, lo, lo + P, y_head, 0)
-        scatter(0, 0, HEAD, y_head)
-        y_all = keep.tile([P, S], F32, name="y_all")
-        product(1, 0, 512, y_all, 0)
-        product(1, 512, S, y_all, 0)
-        scatter(1, 0, S, y_all)
-        store(1)
-        y_rest = keep.tile([P, S - HEAD], F32, name="y_rest")
-        product(0, HEAD, 512, y_rest, HEAD)
-        product(0, 512, S, y_rest, HEAD)
-        scatter(0, HEAD, S, y_rest)
-        store(0)
+        heads = [reuse.tile([P, HEAD], F32, name="y_head0", offset=SECOND, align_bytes=64), keep.tile([P, HEAD], F32, name="y_head1")]
+        for b in range(2):
+            for lo in range(0, HEAD, P):
+                product(b, lo, lo + P, heads[b], 0)
+            scatter(b, 0, HEAD, heads[b])
+        for b in range(2):
+            rest = keep.tile([P, S - HEAD], F32, name=f"y_rest{b}")
+            product(b, HEAD, 512, rest, HEAD)
+            product(b, 512, S, rest, HEAD)
+            scatter(b, HEAD, S, rest)
+            store(b)

@@ -61,18 +61,20 @@ def tile_picked_route2_linnone_p_kernel(tc, x_words, x_scales, gate, w1, offs, d
         nc.sync.dma_start(words[:], x_words[0].rearrange("p c t -> p (c t)").bitcast(I32))
         back0 = load_weights(0, 2, reuse.tile([P, 2, P], F32, name="w_back0", offset=4 * T, align_bytes=64))
         back1 = load_weights(1, 1, reuse.tile([P, 3, P], F32, name="w_back1", offset=SECOND, align_bytes=64))
-        nc.sync.dma_start(dst_sb[:], dst)
 
         nc.vector.memset(x_plane[:].bitcast(I32), 0)
-        nc.vector.memset(windows[0][:, SEED:U], 0.0)
+        nc.vector.memset(windows[0][:, SEED:U // 2], 0.0)
         interleave_weights(0, 0, 2, front[:, 0:3:2, :])
         interleave_weights(1, 0, 1, front[:, 1:2, :])
         nc.scalar.copy(windows[1][:].rearrange("p (a c) -> p a c", c=SEED), windows[0][:, 0:SEED].unsqueeze(1).to_broadcast([P, U // SEED, SEED]))
+
+        nc.scalar.copy(windows[0][:, U // 2:U].rearrange("p (a c) -> p a c", c=SEED), windows[0][:, 0:SEED].unsqueeze(1).to_broadcast([P, U // 2 // SEED, SEED]))
 
         picked = keep.tile([P, S], U8, name="picked", align_bytes=64)
         nc.vector.tensor_copy(picked[:], scales[:].indirect(offs_sb[:]))
         for r in range(4):
             nc.sync.dma_start(x_plane[r:P:32, :].bitcast(I32), picked[ROW0 + r:P:4, :].bitcast(I32))
+        nc.sync.dma_start(dst_sb[:], dst)
         gate_sb = keep.tile([P, S], F32, name="gate_sb", tag="scales_then_gate", align_bytes=64)
         nc.sync.dma_start(gate_sb[:, 0:HEAD], gate[:, 0:HEAD])
         nc.sync.dma_start(gate_sb[:, HEAD:S], gate[:, HEAD:S])

@@ -53,7 +53,7 @@ def tile_picked_route2_linnone_p_kernel(tc, x_words, x_scales, gate, w1, offs, d
 
         nc.vector.memset(windows[0][:, 0:SEED], 0.0)
         nc.vector.memset(scales[0:ROW0, :].bitcast(I32), 0)
-        nc.sync.dma_start(scales[ROW0:P, :].bitcast(I32), x_scales[0].bitcast(I32))
+        nc.scalar.dma_start(scales[ROW0:P, :].bitcast(I32), x_scales[0].bitcast(I32))
         nc.sync.dma_start(offs_sb[:], offs)
         front = keep.tile([P, 3, P], F32, name="w_front", align_bytes=64)
         nc.sync.dma_start(front[:].rearrange("p a m -> p (a m)"), w_rows.rearrange("p j m -> p (j m)")[:, 0:3 * P])

@@ -6,10 +6,9 @@ K, T, S, N, U = 512, 4096, 1024, 256, 2048
 P = 128
 PACK = 4
 FLOPS = 2 * K * N * S
-HEAD = 256
+PIECE = 256
 SEED = 64
 ROW0 = 112
-SECOND = 4 * T + 2048
 
 F32 = mybir.dt.float32
 BF16 = mybir.dt.bfloat16
@@ -19,35 +18,18 @@ U16 = mybir.dt.uint16
 U8 = mybir.dt.uint8
 FP8X4 = mybir.dt.float8_e4m3fn_x4
 MULT = mybir.AluOpType.mult
+COPY = mybir.ActivationFunctionType.Copy
 
 
 def tile_picked_route2_linnone_p_kernel(tc, x_words, x_scales, gate, w1, offs, dst, out):
     nc = tc.nc
     with ExitStack() as ctx:
         keep = ctx.enter_context(tc.tile_pool(name="keep", bufs=1))
-        reuse = ctx.enter_context(tc.tile_pool(name="reuse", bufs=1))
         psum = ctx.enter_context(tc.psum_pool(name="psum", bufs=1))
 
         offs_sb = keep.tile([P, S // 16], U16, name="offs_sb")
         dst_sb = keep.tile([P, S // 16], U16, name="dst_sb")
         windows = [keep.tile([P, U], F32, name=f"window{b}") for b in range(2)]
-        w_rows = w1.rearrange("(p j) m -> p j m", j=PACK)
-
-        grouped = [keep.tile([P, P, PACK], BF16, name=f"w_grouped{b}", align_bytes=64) for b in range(2)]
-
-        def load_weights(b, j, raw):
-            nc.sync.dma_start(raw[:], w_rows[:, j:PACK, b * P:(b + 1) * P])
-            return raw
-
-        def interleave_weights(b, j0, j1, raw):
-            nc.scalar.copy(grouped[b][:, :, j0:j1], raw.rearrange("p j m -> p m j"))
-
-        def quantize_weights(b):
-            codes = keep.tile([P, P], U32, name=f"w_codes{b}", align_bytes=64)
-            plane = keep.tile([P, P], U8, name=f"w_plane{b}", align_bytes=64)
-            nc.vector.quantize_mx(out=codes[:].bitcast(FP8X4), scales=plane[:], in_=grouped[b][:].rearrange("p m j -> p (m j)"))
-            return codes, plane
-
         scales = keep.tile([P, T], U8, name="scales", tag="scales_then_gate", align_bytes=64)
         x_plane = keep.tile([P, S], U8, name="x_plane", align_bytes=64)
 
@@ -55,68 +37,79 @@ def tile_picked_route2_linnone_p_kernel(tc, x_words, x_scales, gate, w1, offs, d
         nc.vector.memset(scales[0:ROW0, :].bitcast(I32), 0)
         nc.scalar.dma_start(scales[ROW0:P, :].bitcast(I32), x_scales[0].bitcast(I32))
         nc.sync.dma_start(offs_sb[:], offs)
-        front = keep.tile([P, 3, P], F32, name="w_front", align_bytes=64)
-        nc.sync.dma_start(front[:].rearrange("p a m -> p (a m)"), w_rows.rearrange("p j m -> p (j m)")[:, 0:3 * P])
-        words = reuse.tile([P, T], I32, name="words", offset=0, align_bytes=64)
+        w_raw = keep.tile([P, PACK, N], F32, name="w_raw", align_bytes=64)
+        nc.sync.dma_start(w_raw[:], w1.rearrange("(p j) m -> p j m", j=PACK))
+        words = keep.tile([P, T], I32, name="words", align_bytes=64)
         nc.sync.dma_start(words[:], x_words[0].rearrange("p c t -> p (c t)").bitcast(I32))
-        back0 = load_weights(0, 2, reuse.tile([P, 2, P], F32, name="w_back0", offset=4 * T, align_bytes=64))
-        back1 = load_weights(1, 1, reuse.tile([P, 3, P], F32, name="w_back1", offset=SECOND, align_bytes=64))
+        nc.sync.dma_start(dst_sb[:], dst)
 
         nc.vector.memset(x_plane[:].bitcast(I32), 0)
         nc.vector.memset(windows[0][:, SEED:U // 2], 0.0)
-        interleave_weights(0, 0, 2, front[:, 0:3:2, :])
-        interleave_weights(1, 0, 1, front[:, 1:2, :])
-        nc.scalar.copy(windows[1][:].rearrange("p (a c) -> p a c", c=SEED), windows[0][:, 0:SEED].unsqueeze(1).to_broadcast([P, U // SEED, SEED]))
+        grouped = keep.tile([P, N, PACK], BF16, name="w_grouped", align_bytes=64)
+        nc.scalar.copy(grouped[:], w_raw[:].rearrange("p j m -> p m j"))
 
-        nc.scalar.copy(windows[0][:, U // 2:U].rearrange("p (a c) -> p a c", c=SEED), windows[0][:, 0:SEED].unsqueeze(1).to_broadcast([P, U // 2 // SEED, SEED]))
+        def spread_zeros(part, width):
+            nc.scalar.copy(part.rearrange("p (a c) -> p a c", c=SEED), windows[0][:, 0:SEED].unsqueeze(1).to_broadcast([P, width // SEED, SEED]))
+
+        spread_zeros(windows[0][:, U // 2:U], U // 2)
+        spread_zeros(windows[1][:], U)
 
         picked = keep.tile([P, S], U8, name="picked", align_bytes=64)
         nc.vector.tensor_copy(picked[:], scales[:].indirect(offs_sb[:]))
         for r in range(4):
             nc.sync.dma_start(x_plane[r:P:32, :].bitcast(I32), picked[ROW0 + r:P:4, :].bitcast(I32))
-        nc.sync.dma_start(dst_sb[:], dst)
         gate_sb = keep.tile([P, S], F32, name="gate_sb", tag="scales_then_gate", align_bytes=64)
-        nc.sync.dma_start(gate_sb[:, 0:HEAD], gate[:, 0:HEAD])
-        nc.sync.dma_start(gate_sb[:, HEAD:S], gate[:, HEAD:S])
+        for lo, hi in ((0, PIECE), (PIECE, 2 * PIECE), (2 * PIECE, S)):
+            nc.sync.dma_start(gate_sb[:, lo:hi], gate[:, lo:hi])
 
-        def gather_words(h, codes):
-            nc.vector.tensor_copy(codes[:], words[:].bitcast(U32).indirect(offs_sb[:, 32 * h:32 * (h + 1)]))
+        w_codes = keep.tile([P, N], U32, name="w_codes", align_bytes=64)
+        w_plane = keep.tile([P, N], U8, name="w_plane", align_bytes=64)
+        nc.vector.quantize_mx(out=w_codes[:].bitcast(FP8X4), scales=w_plane[:], in_=grouped[:].rearrange("p m j -> p (m j)"))
+
+        y = [keep.tile([P, S], F32, name=f"y{b}") for b in range(2)]
+
+        def gather_words(i):
+            codes = keep.tile([P, PIECE], U32, name="x_codes", tag="x_codes", bufs=2, align_bytes=64)
+            nc.vector.tensor_copy(codes[:], words[:].bitcast(U32).indirect(offs_sb[:, i * PIECE // 16:(i + 1) * PIECE // 16]))
             return codes
 
-        x_codes = [gather_words(0, keep.tile([P, 512], U32, name="x_codes0", align_bytes=64))]
-        interleave_weights(0, 2, PACK, back0[:])
-        weights = [quantize_weights(0)]
-        x_codes.append(gather_words(1, reuse.tile([P, 512], U32, name="x_codes1", offset=4 * T, align_bytes=64)))
-        interleave_weights(1, 1, PACK, back1[:])
-        weights.append(quantize_weights(1))
-
-        def product(b, lo, hi, y, y0):
-            acc = psum.tile([P, hi - lo], F32, name="acc", tag="acc", bufs=8)
+        def product(b, i, codes):
+            acc = psum.tile([P, PIECE], F32, name="acc", tag="acc", bufs=8)
             nc.tensor.matmul_mx(
                 out=acc[:],
-                lhsT=weights[b][0][:].bitcast(FP8X4),
-                lhsT_scale=weights[b][1][:],
-                rhs=x_codes[lo // 512][:, lo % 512:lo % 512 + hi - lo].bitcast(FP8X4),
-                rhs_scale=x_plane[:, lo:hi],
+                lhsT=w_codes[:, b * P:(b + 1) * P].bitcast(FP8X4),
+                lhsT_scale=w_plane[:, b * P:(b + 1) * P],
+                rhs=codes[:].bitcast(FP8X4),
+                rhs_scale=x_plane[:, i * PIECE:(i + 1) * PIECE],
                 start=True,
                 stop=True,
             )
-            nc.scalar.copy(y[:, lo - y0:hi - y0], acc[:])
+            return acc
 
-        def scatter(b, lo, hi, y):
-            nc.vector.tensor_tensor(windows[b][:].indirect(dst_sb[:, lo // 16:hi // 16]), y[:], gate_sb[:, lo:hi], MULT)
+        def gated(b, i, acc):
+            cols = slice(i * PIECE, (i + 1) * PIECE)
+            nc.vector.tensor_tensor(y[b][:, cols], acc[:], gate_sb[:, cols], MULT)
 
-        def store(b):
-            nc.sync.dma_start(out[b * P:(b + 1) * P, :], windows[b][:])
+        def ungated(b, i, acc):
+            nc.scalar.copy(y[b][:, i * PIECE:(i + 1) * PIECE], acc[:])
 
-        heads = [reuse.tile([P, HEAD], F32, name="y_head0", offset=SECOND, align_bytes=64), keep.tile([P, HEAD], F32, name="y_head1")]
-        for b in range(2):
-            for lo in range(0, HEAD, P):
-                product(b, lo, lo + P, heads[b], 0)
-            scatter(b, 0, HEAD, heads[b])
-        for b in range(2):
-            rest = keep.tile([P, S - HEAD], F32, name=f"y_rest{b}")
-            product(b, HEAD, 512, rest, HEAD)
-            product(b, 512, S, rest, HEAD)
-            scatter(b, HEAD, S, rest)
-            store(b)
+        def scalar_scatter(i):
+            nc.scalar.activation(windows[0][:].indirect(dst_sb[:, i * PIECE // 16:(i + 1) * PIECE // 16]), y[0][:, i * PIECE:(i + 1) * PIECE], COPY)
+
+        codes = [gather_words(0), gather_words(1)]
+        for i in range(2):
+            accs = [product(b, i, codes[i]) for b in range(2)]
+            gated(0, i, accs[0])
+            ungated(1, i, accs[1])
+            scalar_scatter(i)
+            codes.append(gather_words(i + 2))
+        for i, order in ((2, (0, 1)), (3, (1, 0))):
+            for b in order:
+                gated(b, i, product(b, i, codes[i]))
+            scalar_scatter(i)
+        nc.sync.dma_start(out[0:P, :], windows[0][:])
+
+        half = S // 2
+        nc.vector.tensor_copy(windows[1][:].indirect(dst_sb[:, half // 16:S // 16]), y[1][:, half:S])
+        nc.vector.tensor_tensor(windows[1][:].indirect(dst_sb[:, 0:half // 16]), y[1][:, 0:half], gate_sb[:, 0:half], MULT)
+        nc.sync.dma_start(out[P:N, :], windows[1][:])

@@ -25,28 +25,43 @@ def tile_picked_route2_linnone_p_kernel(tc, x_words, x_scales, gate, w1, offs, d
     nc = tc.nc
     with ExitStack() as ctx:
         keep = ctx.enter_context(tc.tile_pool(name="keep", bufs=1))
+        reuse = ctx.enter_context(tc.tile_pool(name="reuse", bufs=1))
         psum = ctx.enter_context(tc.psum_pool(name="psum", bufs=1))
 
         offs_sb = keep.tile([P, S // 16], U16, name="offs_sb")
         dst_sb = keep.tile([P, S // 16], U16, name="dst_sb")
         windows = [keep.tile([P, U], F32, name=f"window{b}") for b in range(2)]
-        scales = keep.tile([P, T], U8, name="scales", tag="scales_then_gate", align_bytes=64)
+        scales = reuse.tile([P, T], U8, name="scales", offset=0, align_bytes=64)
         x_plane = keep.tile([P, S], U8, name="x_plane", align_bytes=64)
 
         nc.vector.memset(windows[0][:, 0:SEED], 0.0)
         nc.vector.memset(scales[0:ROW0, :].bitcast(I32), 0)
         nc.scalar.dma_start(scales[ROW0:P, :].bitcast(I32), x_scales[0].bitcast(I32))
         nc.sync.dma_start(offs_sb[:], offs)
-        w_raw = keep.tile([P, PACK, N], F32, name="w_raw", align_bytes=64)
-        nc.sync.dma_start(w_raw[:], w1.rearrange("(p j) m -> p j m", j=PACK))
+        w_rows = w1.rearrange("(p j) m -> p j m", j=PACK)
+
+        def load_weights(b, raw):
+            nc.sync.dma_start(raw[:], w_rows[:, :, b * P:(b + 1) * P])
+            return raw
+
+        def interleave(raw, grouped):
+            nc.scalar.copy(grouped[:], raw[:].rearrange("p j m -> p m j"))
+            return grouped
+
+        def quantize_weights(b, grouped):
+            w_codes = keep.tile([P, P], U32, name=f"w_codes{b}", align_bytes=64)
+            w_plane = keep.tile([P, P], U8, name=f"w_plane{b}", align_bytes=64)
+            nc.vector.quantize_mx(out=w_codes[:].bitcast(FP8X4), scales=w_plane[:], in_=grouped[:].rearrange("p m j -> p (m j)"))
+            return w_codes, w_plane
+
+        raw0 = load_weights(0, keep.tile([P, PACK, P], F32, name="w_raw0", align_bytes=64))
         words = keep.tile([P, T], I32, name="words", align_bytes=64)
         nc.sync.dma_start(words[:], x_words[0].rearrange("p c t -> p (c t)").bitcast(I32))
         nc.sync.dma_start(dst_sb[:], dst)
 
         nc.vector.memset(x_plane[:].bitcast(I32), 0)
         nc.vector.memset(windows[0][:, SEED:U // 2], 0.0)
-        grouped = keep.tile([P, N, PACK], BF16, name="w_grouped", align_bytes=64)
-        nc.scalar.copy(grouped[:], w_raw[:].rearrange("p j m -> p m j"))
+        grouped0 = interleave(raw0, keep.tile([P, P, PACK], BF16, name="w_grouped0", align_bytes=64))
 
         def spread_zeros(part, width):
             nc.scalar.copy(part.rearrange("p (a c) -> p a c", c=SEED), windows[0][:, 0:SEED].unsqueeze(1).to_broadcast([P, width // SEED, SEED]))
@@ -58,58 +73,70 @@ def tile_picked_route2_linnone_p_kernel(tc, x_words, x_scales, gate, w1, offs, d
         nc.vector.tensor_copy(picked[:], scales[:].indirect(offs_sb[:]))
         for r in range(4):
             nc.sync.dma_start(x_plane[r:P:32, :].bitcast(I32), picked[ROW0 + r:P:4, :].bitcast(I32))
-        gate_sb = keep.tile([P, S], F32, name="gate_sb", tag="scales_then_gate", align_bytes=64)
-        for lo, hi in ((0, PIECE), (PIECE, 2 * PIECE), (2 * PIECE, S)):
-            nc.sync.dma_start(gate_sb[:, lo:hi], gate[:, lo:hi])
+        raw1 = load_weights(1, reuse.tile([P, PACK, P], F32, name="w_raw1", offset=0, align_bytes=64))
+        gate_sb = reuse.tile([P, S], F32, name="gate_sb", offset=T // 2, align_bytes=64)
+        nc.sync.dma_start(gate_sb[:, 0:PIECE], gate[:, 0:PIECE])
+        nc.sync.dma_start(gate_sb[:, PIECE:S], gate[:, PIECE:S])
 
-        w_codes = keep.tile([P, N], U32, name="w_codes", align_bytes=64)
-        w_plane = keep.tile([P, N], U8, name="w_plane", align_bytes=64)
-        nc.vector.quantize_mx(out=w_codes[:].bitcast(FP8X4), scales=w_plane[:], in_=grouped[:].rearrange("p m j -> p (m j)"))
+        weights = [quantize_weights(0, grouped0)]
 
-        y = [keep.tile([P, S], F32, name=f"y{b}") for b in range(2)]
-
-        def gather_words(i):
-            codes = keep.tile([P, PIECE], U32, name="x_codes", tag="x_codes", bufs=2, align_bytes=64)
+        def gather_words(i, codes):
             nc.vector.tensor_copy(codes[:], words[:].bitcast(U32).indirect(offs_sb[:, i * PIECE // 16:(i + 1) * PIECE // 16]))
             return codes
 
-        def product(b, i, codes):
-            acc = psum.tile([P, PIECE], F32, name="acc", tag="acc", bufs=8)
+        def bank(width):
+            return psum.tile([P, width], F32, name="acc", tag="acc", bufs=8)
+
+        def product(b, lo, hi, acc):
             nc.tensor.matmul_mx(
-                out=acc[:],
-                lhsT=w_codes[:, b * P:(b + 1) * P].bitcast(FP8X4),
-                lhsT_scale=w_plane[:, b * P:(b + 1) * P],
-                rhs=codes[:].bitcast(FP8X4),
-                rhs_scale=x_plane[:, i * PIECE:(i + 1) * PIECE],
+                out=acc,
+                lhsT=weights[b][0][:].bitcast(FP8X4),
+                lhsT_scale=weights[b][1][:],
+                rhs=codes[lo // PIECE][:, lo % PIECE:lo % PIECE + hi - lo].bitcast(FP8X4),
+                rhs_scale=x_plane[:, lo:hi],
                 start=True,
                 stop=True,
             )
+
+        def products(b, lo, hi):
+            acc = bank(hi - lo)
+            cuts = [lo] + [c for c in range(PIECE, S, PIECE) if lo < c < hi] + [hi]
+            for c0, c1 in zip(cuts, cuts[1:]):
+                product(b, c0, c1, acc[:, c0 - lo:c1 - lo])
             return acc
 
-        def gated(b, i, acc):
-            cols = slice(i * PIECE, (i + 1) * PIECE)
-            nc.vector.tensor_tensor(y[b][:, cols], acc[:], gate_sb[:, cols], MULT)
+        def gated(b, lo, hi, y):
+            nc.vector.tensor_tensor(y, products(b, lo, hi)[:], gate_sb[:, lo:hi], MULT)
 
-        def ungated(b, i, acc):
-            nc.scalar.copy(y[b][:, i * PIECE:(i + 1) * PIECE], acc[:])
+        def ungated(lo, hi, y):
+            nc.scalar.copy(y, products(1, lo, hi)[:])
 
-        def scalar_scatter(i):
-            nc.scalar.activation(windows[0][:].indirect(dst_sb[:, i * PIECE // 16:(i + 1) * PIECE // 16]), y[0][:, i * PIECE:(i + 1) * PIECE], COPY)
+        def scalar_scatter(lo, hi, y):
+            nc.scalar.activation(windows[0][:].indirect(dst_sb[:, lo // 16:hi // 16]), y, COPY)
 
-        codes = [gather_words(0), gather_words(1)]
-        for i in range(2):
-            accs = [product(b, i, codes[i]) for b in range(2)]
-            gated(0, i, accs[0])
-            ungated(1, i, accs[1])
-            scalar_scatter(i)
-            codes.append(gather_words(i + 2))
-        for i, order in ((2, (0, 1)), (3, (1, 0))):
-            for b in order:
-                gated(b, i, product(b, i, codes[i]))
-            scalar_scatter(i)
+        def copied(lo, hi, y):
+            nc.vector.tensor_copy(y, products(1, lo, hi)[:])
+
+        y0 = keep.tile([P, S], F32, name="y0")
+        y1 = keep.tile([P, S], F32, name="y1")
+
+        codes = [gather_words(i, keep.tile([P, PIECE], U32, name=f"x_codes{i}", align_bytes=64)) for i in range(2)]
+        gated(0, 0, 256, y0[:, 0:256])
+        grouped1 = interleave(raw1, keep.tile([P, P, PACK], BF16, name="w_grouped1", align_bytes=64))
+        scalar_scatter(0, 256, y0[:, 0:256])
+        gated(0, 256, 512, y0[:, 256:512])
+        weights.append(quantize_weights(1, grouped1))
+        for i in (2, 3):
+            codes.append(gather_words(i, reuse.tile([P, PIECE], U32, name=f"x_codes{i}", offset=1024 * (i - 2), align_bytes=64)))
+        copied(0, 256, y1[:, 0:256])
+        ungated(256, 512, y1[:, 256:512])
+        gated(0, 512, 640, y0[:, 512:640])
+        scalar_scatter(256, 640, y0[:, 256:640])
+        nc.vector.tensor_tensor(windows[1][:].indirect(dst_sb[:, 0:16]), y1[:, 0:256], gate_sb[:, 0:256], MULT)
+        copied(512, 1024, y1[:, 512:1024])
+        gated(0, 640, 1024, y0[:, 640:1024])
+        scalar_scatter(640, 1024, y0[:, 640:1024])
         nc.sync.dma_start(out[0:P, :], windows[0][:])
 
-        half = S // 2
-        nc.vector.tensor_copy(windows[1][:].indirect(dst_sb[:, half // 16:S // 16]), y[1][:, half:S])
-        nc.vector.tensor_tensor(windows[1][:].indirect(dst_sb[:, 0:half // 16]), y[1][:, 0:half], gate_sb[:, 0:half], MULT)
+        nc.vector.tensor_tensor(windows[1][:].indirect(dst_sb[:, 16:64]), y1[:, 256:1024], gate_sb[:, 256:1024], MULT)
         nc.sync.dma_start(out[P:N, :], windows[1][:])

@@ -31,7 +31,7 @@ def tile_picked_route2_linnone_p_kernel(tc, x_words, x_scales, gate, w1, offs, d
         offs_sb = keep.tile([P, S // 16], U16, name="offs_sb")
         dst_sb = keep.tile([P, S // 16], U16, name="dst_sb")
         windows = [keep.tile([P, U], F32, name=f"window{b}") for b in range(2)]
-        scales = reuse.tile([P, T], U8, name="scales", offset=0, align_bytes=64)
+        scales = reuse.tile([P, T], U8, name="scales", offset=2048, align_bytes=64)
         x_plane = keep.tile([P, S], U8, name="x_plane", align_bytes=64)
 
         nc.vector.memset(windows[0][:, 0:SEED], 0.0)
@@ -73,8 +73,8 @@ def tile_picked_route2_linnone_p_kernel(tc, x_words, x_scales, gate, w1, offs, d
         nc.vector.tensor_copy(picked[:], scales[:].indirect(offs_sb[:]))
         for r in range(4):
             nc.sync.dma_start(x_plane[r:P:32, :].bitcast(I32), picked[ROW0 + r:P:4, :].bitcast(I32))
-        raw1 = load_weights(1, reuse.tile([P, PACK, P], F32, name="w_raw1", offset=0, align_bytes=64))
-        gate_sb = reuse.tile([P, S], F32, name="gate_sb", offset=T // 2, align_bytes=64)
+        raw1 = load_weights(1, reuse.tile([P, PACK, P], F32, name="w_raw1", offset=1472, align_bytes=64))
+        gate_sb = reuse.tile([P, S], F32, name="gate_sb", offset=3584, align_bytes=64)
         nc.sync.dma_start(gate_sb[:, 0:PIECE], gate[:, 0:PIECE])
         nc.sync.dma_start(gate_sb[:, PIECE:S], gate[:, PIECE:S])
 
@@ -117,25 +117,31 @@ def tile_picked_route2_linnone_p_kernel(tc, x_words, x_scales, gate, w1, offs, d
         def copied(lo, hi, y):
             nc.vector.tensor_copy(y, products(1, lo, hi)[:])
 
-        y0 = keep.tile([P, S], F32, name="y0")
+        y_first = keep.tile([P, 256], F32, name="y_first")
+        y_last = keep.tile([P, 384], F32, name="y_last")
         y1 = keep.tile([P, S], F32, name="y1")
 
         codes = [gather_words(i, keep.tile([P, PIECE], U32, name=f"x_codes{i}", align_bytes=64)) for i in range(2)]
-        gated(0, 0, 256, y0[:, 0:256])
+        gated(0, 0, 128, y_first[:, 0:128])
+        gated(0, 128, 256, y_first[:, 128:256])
         grouped1 = interleave(raw1, keep.tile([P, P, PACK], BF16, name="w_grouped1", align_bytes=64))
-        scalar_scatter(0, 256, y0[:, 0:256])
-        gated(0, 256, 512, y0[:, 256:512])
+        scalar_scatter(0, 256, y_first[:])
         weights.append(quantize_weights(1, grouped1))
-        for i in (2, 3):
-            codes.append(gather_words(i, reuse.tile([P, PIECE], U32, name=f"x_codes{i}", offset=1024 * (i - 2), align_bytes=64)))
-        copied(0, 256, y1[:, 0:256])
-        ungated(256, 512, y1[:, 256:512])
-        gated(0, 512, 640, y0[:, 512:640])
-        scalar_scatter(256, 640, y0[:, 256:640])
+        codes.append(gather_words(2, reuse.tile([P, PIECE], U32, name="x_codes2", offset=1536, align_bytes=64)))
+        y_mid = reuse.tile([P, 384], F32, name="y_mid", offset=0, align_bytes=64)
+        gated(0, 256, 512, y_mid[:, 0:256])
+        codes.append(gather_words(3, reuse.tile([P, PIECE], U32, name="x_codes3", offset=2560, align_bytes=64)))
+        shared = bank(384)
+        product(1, 0, 256, shared[:, 0:256])
+        product(0, 512, 640, shared[:, 256:384])
+        nc.vector.tensor_tensor(y_mid[:, 256:384], shared[:, 256:384], gate_sb[:, 512:640], MULT)
+        nc.vector.tensor_copy(y1[:, 0:256], shared[:, 0:256])
+        ungated(256, 640, y1[:, 256:640])
+        scalar_scatter(256, 640, y_mid[:])
         nc.vector.tensor_tensor(windows[1][:].indirect(dst_sb[:, 0:16]), y1[:, 0:256], gate_sb[:, 0:256], MULT)
-        copied(512, 1024, y1[:, 512:1024])
-        gated(0, 640, 1024, y0[:, 640:1024])
-        scalar_scatter(640, 1024, y0[:, 640:1024])
+        copied(640, 1024, y1[:, 640:1024])
+        gated(0, 640, 1024, y_last[:])
+        scalar_scatter(640, 1024, y_last[:])
         nc.sync.dma_start(out[0:P, :], windows[0][:])
 
         nc.vector.tensor_tensor(windows[1][:].indirect(dst_sb[:, 16:64]), y1[:, 256:1024], gate_sb[:, 256:1024], MULT)

@@ -9,6 +9,8 @@ FLOPS = 2 * K * N * S
 PIECE = 256
 SEED = 64
 ROW0 = 112
+SHARE = 96
+CUTS = (0, 256, 512, 768, 1024)
 
 F32 = mybir.dt.float32
 BF16 = mybir.dt.bfloat16
@@ -18,6 +20,7 @@ U16 = mybir.dt.uint16
 U8 = mybir.dt.uint8
 FP8X4 = mybir.dt.float8_e4m3fn_x4
 MULT = mybir.AluOpType.mult
+ADD = mybir.AluOpType.add
 COPY = mybir.ActivationFunctionType.Copy
 
 
@@ -31,7 +34,7 @@ def tile_picked_route2_linnone_p_kernel(tc, x_words, x_scales, gate, w1, offs, d
         offs_sb = keep.tile([P, S // 16], U16, name="offs_sb")
         dst_sb = keep.tile([P, S // 16], U16, name="dst_sb")
         windows = [keep.tile([P, U], F32, name=f"window{b}") for b in range(2)]
-        scales = reuse.tile([P, T], U8, name="scales", offset=2048, align_bytes=64)
+        scales = reuse.tile([P, T], U8, name="scales", offset=0, align_bytes=64)
         x_plane = keep.tile([P, S], U8, name="x_plane", align_bytes=64)
 
         nc.vector.memset(windows[0][:, 0:SEED], 0.0)
@@ -45,7 +48,12 @@ def tile_picked_route2_linnone_p_kernel(tc, x_words, x_scales, gate, w1, offs, d
             return raw
 
         def interleave(raw, grouped):
-            nc.scalar.copy(grouped[:], raw[:].rearrange("p j m -> p m j"))
+            nc.scalar.copy(grouped[:].rearrange("p (c i) j -> p c j i", i=4), raw[:].rearrange("p j (c i) -> p c j i", i=4))
+            return grouped
+
+        def interleave_shared(raw, grouped):
+            nc.scalar.copy(grouped[:, 0:SHARE, :].rearrange("p (c i) j -> p c j i", i=4), raw[:, :, 0:SHARE].rearrange("p j (c i) -> p c j i", i=4))
+            nc.gpsimd.tensor_scalar(grouped[:, SHARE:P, :].rearrange("p (c i) j -> p c j i", i=4), raw[:, :, SHARE:P].rearrange("p j (c i) -> p c j i", i=4), 1.0, 0.0, MULT, ADD)
             return grouped
 
         def quantize_weights(b, grouped):
@@ -54,45 +62,42 @@ def tile_picked_route2_linnone_p_kernel(tc, x_words, x_scales, gate, w1, offs, d
             nc.vector.quantize_mx(out=w_codes[:].bitcast(FP8X4), scales=w_plane[:], in_=grouped[:].rearrange("p m j -> p (m j)"))
             return w_codes, w_plane
 
-        raw0 = load_weights(0, keep.tile([P, PACK, P], F32, name="w_raw0", align_bytes=64))
         words = keep.tile([P, T], I32, name="words", align_bytes=64)
         nc.sync.dma_start(words[:], x_words[0].rearrange("p c t -> p (c t)").bitcast(I32))
+        raw0 = load_weights(0, reuse.tile([P, PACK, P], F32, name="w_raw0", offset=8192, align_bytes=64))
         nc.sync.dma_start(dst_sb[:], dst)
 
         nc.vector.memset(x_plane[:].bitcast(I32), 0)
-        nc.vector.memset(windows[0][:, SEED:U // 2], 0.0)
-        grouped0 = interleave(raw0, keep.tile([P, P, PACK], BF16, name="w_grouped0", align_bytes=64))
 
         def spread_zeros(part, width):
             nc.scalar.copy(part.rearrange("p (a c) -> p a c", c=SEED), windows[0][:, 0:SEED].unsqueeze(1).to_broadcast([P, width // SEED, SEED]))
 
-        spread_zeros(windows[0][:, U // 2:U], U // 2)
+        spread_zeros(windows[0][:, SEED:U], U - SEED)
         spread_zeros(windows[1][:], U)
 
         picked = keep.tile([P, S], U8, name="picked", align_bytes=64)
         nc.vector.tensor_copy(picked[:], scales[:].indirect(offs_sb[:]))
         for r in range(4):
             nc.sync.dma_start(x_plane[r:P:32, :].bitcast(I32), picked[ROW0 + r:P:4, :].bitcast(I32))
-        raw1 = load_weights(1, reuse.tile([P, PACK, P], F32, name="w_raw1", offset=1472, align_bytes=64))
-        gate_sb = reuse.tile([P, S], F32, name="gate_sb", offset=3584, align_bytes=64)
+        gate_sb = reuse.tile([P, S], F32, name="gate_sb", offset=2048, align_bytes=64)
+        raw1 = load_weights(1, reuse.tile([P, PACK, P], F32, name="w_raw1", offset=0, align_bytes=64))
         nc.sync.dma_start(gate_sb[:, 0:PIECE], gate[:, 0:PIECE])
         nc.sync.dma_start(gate_sb[:, PIECE:S], gate[:, PIECE:S])
 
-        weights = [quantize_weights(0, grouped0)]
-
         def gather_words(i, codes):
-            nc.vector.tensor_copy(codes[:], words[:].bitcast(U32).indirect(offs_sb[:, i * PIECE // 16:(i + 1) * PIECE // 16]))
+            nc.vector.tensor_copy(codes[:], words[:].bitcast(U32).indirect(offs_sb[:, CUTS[i] // 16:CUTS[i + 1] // 16]))
             return codes
 
         def bank(width):
             return psum.tile([P, width], F32, name="acc", tag="acc", bufs=8)
 
         def product(b, lo, hi, acc):
+            i = max(g for g in range(4) if CUTS[g] <= lo)
             nc.tensor.matmul_mx(
                 out=acc,
                 lhsT=weights[b][0][:].bitcast(FP8X4),
                 lhsT_scale=weights[b][1][:],
-                rhs=codes[lo // PIECE][:, lo % PIECE:lo % PIECE + hi - lo].bitcast(FP8X4),
+                rhs=codes[i][:, lo - CUTS[i]:hi - CUTS[i]].bitcast(FP8X4),
                 rhs_scale=x_plane[:, lo:hi],
                 start=True,
                 stop=True,
@@ -100,7 +105,7 @@ def tile_picked_route2_linnone_p_kernel(tc, x_words, x_scales, gate, w1, offs, d
 
         def products(b, lo, hi):
             acc = bank(hi - lo)
-            cuts = [lo] + [c for c in range(PIECE, S, PIECE) if lo < c < hi] + [hi]
+            cuts = [lo] + [c for c in CUTS if lo < c < hi] + [hi]
             for c0, c1 in zip(cuts, cuts[1:]):
                 product(b, c0, c1, acc[:, c0 - lo:c1 - lo])
             return acc
@@ -117,31 +122,30 @@ def tile_picked_route2_linnone_p_kernel(tc, x_words, x_scales, gate, w1, offs, d
         def copied(lo, hi, y):
             nc.vector.tensor_copy(y, products(1, lo, hi)[:])
 
-        y_first = keep.tile([P, 256], F32, name="y_first")
-        y_last = keep.tile([P, 384], F32, name="y_last")
+        y0 = keep.tile([P, S], F32, name="y0")
         y1 = keep.tile([P, S], F32, name="y1")
 
-        codes = [gather_words(i, keep.tile([P, PIECE], U32, name=f"x_codes{i}", align_bytes=64)) for i in range(2)]
-        gated(0, 0, 128, y_first[:, 0:128])
-        gated(0, 128, 256, y_first[:, 128:256])
+        codes = [gather_words(i, keep.tile([P, 256], U32, name=f"x_codes{i}", align_bytes=64)) for i in range(2)]
+        grouped0 = interleave_shared(raw0, keep.tile([P, P, PACK], BF16, name="w_grouped0", align_bytes=64))
+        weights = [quantize_weights(0, grouped0)]
+        codes.append(gather_words(2, reuse.tile([P, 256], U32, name="x_codes2", offset=8192, align_bytes=64)))
+        gated(0, 0, 256, y0[:, 0:256])
         grouped1 = interleave(raw1, keep.tile([P, P, PACK], BF16, name="w_grouped1", align_bytes=64))
-        scalar_scatter(0, 256, y_first[:])
+        scalar_scatter(0, 256, y0[:, 0:256])
+        gated(0, 256, 512, y0[:, 256:512])
         weights.append(quantize_weights(1, grouped1))
-        codes.append(gather_words(2, reuse.tile([P, PIECE], U32, name="x_codes2", offset=1536, align_bytes=64)))
-        y_mid = reuse.tile([P, 384], F32, name="y_mid", offset=0, align_bytes=64)
-        gated(0, 256, 512, y_mid[:, 0:256])
-        codes.append(gather_words(3, reuse.tile([P, PIECE], U32, name="x_codes3", offset=2560, align_bytes=64)))
+        codes.append(gather_words(3, reuse.tile([P, 256], U32, name="x_codes3", offset=0, align_bytes=64)))
         shared = bank(384)
-        product(1, 0, 256, shared[:, 0:256])
         product(0, 512, 640, shared[:, 256:384])
-        nc.vector.tensor_tensor(y_mid[:, 256:384], shared[:, 256:384], gate_sb[:, 512:640], MULT)
+        product(1, 0, 256, shared[:, 0:256])
         nc.vector.tensor_copy(y1[:, 0:256], shared[:, 0:256])
-        ungated(256, 640, y1[:, 256:640])
-        scalar_scatter(256, 640, y_mid[:])
+        ungated(256, 512, y1[:, 256:512])
+        nc.vector.tensor_tensor(y0[:, 512:640], shared[:, 256:384], gate_sb[:, 512:640], MULT)
+        scalar_scatter(256, 640, y0[:, 256:640])
         nc.vector.tensor_tensor(windows[1][:].indirect(dst_sb[:, 0:16]), y1[:, 0:256], gate_sb[:, 0:256], MULT)
-        copied(640, 1024, y1[:, 640:1024])
-        gated(0, 640, 1024, y_last[:])
-        scalar_scatter(640, 1024, y_last[:])
+        copied(512, 1024, y1[:, 512:1024])
+        gated(0, 640, 1024, y0[:, 640:1024])
+        scalar_scatter(640, 1024, y0[:, 640:1024])
         nc.sync.dma_start(out[0:P, :], windows[0][:])
 
         nc.vector.tensor_tensor(windows[1][:].indirect(dst_sb[:, 16:64]), y1[:, 256:1024], gate_sb[:, 256:1024], MULT)

@@ -113,9 +113,6 @@ def tile_picked_route2_linnone_p_kernel(tc, x_words, x_scales, gate, w1, offs, d
         def gated(b, lo, hi, y):
             nc.vector.tensor_tensor(y, products(b, lo, hi)[:], gate_sb[:, lo:hi], MULT)
 
-        def ungated(lo, hi, y):
-            nc.scalar.copy(y, products(1, lo, hi)[:])
-
         def scalar_scatter(lo, hi, y):
             nc.scalar.activation(windows[0][:].indirect(dst_sb[:, lo // 16:hi // 16]), y, COPY)
 
@@ -132,21 +129,15 @@ def tile_picked_route2_linnone_p_kernel(tc, x_words, x_scales, gate, w1, offs, d
         gated(0, 0, 256, y0[:, 0:256])
         grouped1 = interleave(raw1, keep.tile([P, P, PACK], BF16, name="w_grouped1", align_bytes=64))
         scalar_scatter(0, 256, y0[:, 0:256])
-        gated(0, 256, 512, y0[:, 256:512])
         weights.append(quantize_weights(1, grouped1))
+        gated(0, 256, 640, y0[:, 256:640])
         codes.append(gather_words(3, reuse.tile([P, 256], U32, name="x_codes3", offset=0, align_bytes=64)))
-        shared = bank(384)
-        product(0, 512, 640, shared[:, 256:384])
-        product(1, 0, 256, shared[:, 0:256])
-        nc.vector.tensor_copy(y1[:, 0:256], shared[:, 0:256])
-        ungated(256, 512, y1[:, 256:512])
-        nc.vector.tensor_tensor(y0[:, 512:640], shared[:, 256:384], gate_sb[:, 512:640], MULT)
         scalar_scatter(256, 640, y0[:, 256:640])
-        nc.vector.tensor_tensor(windows[1][:].indirect(dst_sb[:, 0:16]), y1[:, 0:256], gate_sb[:, 0:256], MULT)
+        copied(0, 512, y1[:, 0:512])
         copied(512, 1024, y1[:, 512:1024])
         gated(0, 640, 1024, y0[:, 640:1024])
         scalar_scatter(640, 1024, y0[:, 640:1024])
         nc.sync.dma_start(out[0:P, :], windows[0][:])
 
-        nc.vector.tensor_tensor(windows[1][:].indirect(dst_sb[:, 16:64]), y1[:, 256:1024], gate_sb[:, 256:1024], MULT)
+        nc.vector.tensor_tensor(windows[1][:].indirect(dst_sb[:]), y1[:], gate_sb[:], MULT)
         nc.sync.dma_start(out[P:N, :], windows[1][:])

@@ -126,7 +126,8 @@ def tile_picked_route2_linnone_p_kernel(tc, x_words, x_scales, gate, w1, offs, d
         grouped0 = interleave_shared(raw0, keep.tile([P, P, PACK], BF16, name="w_grouped0", align_bytes=64))
         weights = [quantize_weights(0, grouped0)]
         codes.append(gather_words(2, reuse.tile([P, 256], U32, name="x_codes2", offset=8192, align_bytes=64)))
-        gated(0, 0, 256, y0[:, 0:256])
+        gated(0, 0, P, y0[:, 0:P])
+        gated(0, P, 256, y0[:, P:256])
         grouped1 = interleave(raw1, keep.tile([P, P, PACK], BF16, name="w_grouped1", align_bytes=64))
         scalar_scatter(0, 256, y0[:, 0:256])
         weights.append(quantize_weights(1, grouped1))

@@ -47,10 +47,6 @@ def tile_picked_route2_linnone_p_kernel(tc, x_words, x_scales, gate, w1, offs, d
             nc.sync.dma_start(raw[:], w_rows[:, :, b * P:(b + 1) * P])
             return raw
 
-        def interleave(raw, grouped):
-            nc.scalar.copy(grouped[:].rearrange("p (c i) j -> p c j i", i=4), raw[:].rearrange("p j (c i) -> p c j i", i=4))
-            return grouped
-
         def interleave_shared(raw, grouped):
             nc.scalar.copy(grouped[:, 0:SHARE, :].rearrange("p (c i) j -> p c j i", i=4), raw[:, :, 0:SHARE].rearrange("p j (c i) -> p c j i", i=4))
             nc.gpsimd.tensor_scalar(grouped[:, SHARE:P, :].rearrange("p (c i) j -> p c j i", i=4), raw[:, :, SHARE:P].rearrange("p j (c i) -> p c j i", i=4), 1.0, 0.0, MULT, ADD)
@@ -128,7 +124,7 @@ def tile_picked_route2_linnone_p_kernel(tc, x_words, x_scales, gate, w1, offs, d
         codes.append(gather_words(2, reuse.tile([P, 256], U32, name="x_codes2", offset=8192, align_bytes=64)))
         gated(0, 0, P, y0[:, 0:P])
         gated(0, P, 256, y0[:, P:256])
-        grouped1 = interleave(raw1, keep.tile([P, P, PACK], BF16, name="w_grouped1", align_bytes=64))
+        grouped1 = interleave_shared(raw1, keep.tile([P, P, PACK], BF16, name="w_grouped1", align_bytes=64))
         scalar_scatter(0, 256, y0[:, 0:256])
         weights.append(quantize_weights(1, grouped1))
         gated(0, 256, 640, y0[:, 256:640])

@@ -9,7 +9,7 @@ FLOPS = 2 * K * N * S
 PIECE = 256
 SEED = 64
 ROW0 = 112
-SHARE = 96
+SHARE = 80
 CUTS = (0, 256, 512, 768, 1024)
 
 F32 = mybir.dt.float32

@@ -6,11 +6,6 @@ K, T, S, N, U = 512, 4096, 1024, 256, 2048
 P = 128
 PACK = 4
 FLOPS = 2 * K * N * S
-PIECE = 256
-SEED = 64
-ROW0 = 112
-SHARE = 80
-CUTS = (0, 256, 512, 768, 1024)
 
 F32 = mybir.dt.float32
 BF16 = mybir.dt.bfloat16
@@ -22,6 +17,16 @@ FP8X4 = mybir.dt.float8_e4m3fn_x4
 MULT = mybir.AluOpType.mult
 ADD = mybir.AluOpType.add
 COPY = mybir.ActivationFunctionType.Copy
+
+GATHER = 256
+FIRST = 256
+HEAD = 256
+LONG = 384
+TAIL = 704
+SEED = 64
+ROW0 = 112
+SHARE = 80
+WIDTHS = (256, 128, 64)
 
 
 def tile_picked_route2_linnone_p_kernel(tc, x_words, x_scales, gate, w1, offs, dst, out):
@@ -36,33 +41,19 @@ def tile_picked_route2_linnone_p_kernel(tc, x_words, x_scales, gate, w1, offs, d
         windows = [keep.tile([P, U], F32, name=f"window{b}") for b in range(2)]
         scales = reuse.tile([P, T], U8, name="scales", offset=0, align_bytes=64)
         x_plane = keep.tile([P, S], U8, name="x_plane", align_bytes=64)
+        words = keep.tile([P, T], I32, name="words", align_bytes=64)
+        picked = keep.tile([P, S], U8, name="picked", align_bytes=64)
+        y = [keep.tile([P, S], F32, name=f"y{b}") for b in range(2)]
+        w_rows = w1.rearrange("(p j) m -> p j m", j=PACK)
 
         nc.vector.memset(windows[0][:, 0:SEED], 0.0)
         nc.vector.memset(scales[0:ROW0, :].bitcast(I32), 0)
         nc.scalar.dma_start(scales[ROW0:P, :].bitcast(I32), x_scales[0].bitcast(I32))
         nc.sync.dma_start(offs_sb[:], offs)
-        w_rows = w1.rearrange("(p j) m -> p j m", j=PACK)
-
-        def load_weights(b, raw):
-            nc.sync.dma_start(raw[:], w_rows[:, :, b * P:(b + 1) * P])
-            return raw
-
-        def interleave_shared(raw, grouped):
-            nc.scalar.copy(grouped[:, 0:SHARE, :].rearrange("p (c i) j -> p c j i", i=4), raw[:, :, 0:SHARE].rearrange("p j (c i) -> p c j i", i=4))
-            nc.gpsimd.tensor_scalar(grouped[:, SHARE:P, :].rearrange("p (c i) j -> p c j i", i=4), raw[:, :, SHARE:P].rearrange("p j (c i) -> p c j i", i=4), 1.0, 0.0, MULT, ADD)
-            return grouped
-
-        def quantize_weights(b, grouped):
-            w_codes = keep.tile([P, P], U32, name=f"w_codes{b}", align_bytes=64)
-            w_plane = keep.tile([P, P], U8, name=f"w_plane{b}", align_bytes=64)
-            nc.vector.quantize_mx(out=w_codes[:].bitcast(FP8X4), scales=w_plane[:], in_=grouped[:].rearrange("p m j -> p (m j)"))
-            return w_codes, w_plane
-
-        words = keep.tile([P, T], I32, name="words", align_bytes=64)
         nc.sync.dma_start(words[:], x_words[0].rearrange("p c t -> p (c t)").bitcast(I32))
-        raw0 = load_weights(0, reuse.tile([P, PACK, P], F32, name="w_raw0", offset=8192, align_bytes=64))
+        raw0 = reuse.tile([P, PACK, P], F32, name="w_raw0", offset=8192, align_bytes=64)
+        nc.sync.dma_start(raw0[:], w_rows[:, :, 0:P])
         nc.sync.dma_start(dst_sb[:], dst)
-
         nc.vector.memset(x_plane[:].bitcast(I32), 0)
 
         def spread_zeros(part, width):
@@ -71,70 +62,75 @@ def tile_picked_route2_linnone_p_kernel(tc, x_words, x_scales, gate, w1, offs, d
         spread_zeros(windows[0][:, SEED:U], U - SEED)
         spread_zeros(windows[1][:], U)
 
-        picked = keep.tile([P, S], U8, name="picked", align_bytes=64)
         nc.vector.tensor_copy(picked[:], scales[:].indirect(offs_sb[:]))
         for r in range(4):
             nc.sync.dma_start(x_plane[r:P:32, :].bitcast(I32), picked[ROW0 + r:P:4, :].bitcast(I32))
+        raw1 = reuse.tile([P, PACK, P], F32, name="w_raw1", offset=0, align_bytes=64)
         gate_sb = reuse.tile([P, S], F32, name="gate_sb", offset=2048, align_bytes=64)
-        raw1 = load_weights(1, reuse.tile([P, PACK, P], F32, name="w_raw1", offset=0, align_bytes=64))
-        nc.sync.dma_start(gate_sb[:, 0:PIECE], gate[:, 0:PIECE])
-        nc.sync.dma_start(gate_sb[:, PIECE:S], gate[:, PIECE:S])
+        nc.sync.dma_start(raw1[:], w_rows[:, :, P:N])
+        nc.sync.dma_start(gate_sb[:, 0:FIRST], gate[:, 0:FIRST])
+        nc.sync.dma_start(gate_sb[:, FIRST:S], gate[:, FIRST:S])
 
-        def gather_words(i, codes):
-            nc.vector.tensor_copy(codes[:], words[:].bitcast(U32).indirect(offs_sb[:, CUTS[i] // 16:CUTS[i + 1] // 16]))
-            return codes
+        def interleave(b, raw):
+            grouped = keep.tile([P, P, PACK], BF16, name=f"w_grouped{b}", align_bytes=64)
+            nc.scalar.copy(grouped[:, 0:SHARE, :].rearrange("p (c i) j -> p c j i", i=4), raw[:, :, 0:SHARE].rearrange("p j (c i) -> p c j i", i=4))
+            nc.gpsimd.tensor_scalar(grouped[:, SHARE:P, :].rearrange("p (c i) j -> p c j i", i=4), raw[:, :, SHARE:P].rearrange("p j (c i) -> p c j i", i=4), 1.0, 0.0, MULT, ADD)
+            return grouped
 
-        def bank(width):
-            return psum.tile([P, width], F32, name="acc", tag="acc", bufs=8)
+        def quantize(b, grouped):
+            w_codes = keep.tile([P, P], U32, name=f"w_codes{b}", align_bytes=64)
+            w_plane = keep.tile([P, P], U8, name=f"w_plane{b}", align_bytes=64)
+            nc.vector.quantize_mx(out=w_codes[:].bitcast(FP8X4), scales=w_plane[:], in_=grouped[:].rearrange("p m j -> p (m j)"))
+            return w_codes, w_plane
 
-        def product(b, lo, hi, acc):
-            i = max(g for g in range(4) if CUTS[g] <= lo)
-            nc.tensor.matmul_mx(
-                out=acc,
-                lhsT=weights[b][0][:].bitcast(FP8X4),
-                lhsT_scale=weights[b][1][:],
-                rhs=codes[i][:, lo - CUTS[i]:hi - CUTS[i]].bitcast(FP8X4),
-                rhs_scale=x_plane[:, lo:hi],
-                start=True,
-                stop=True,
-            )
+        def gather(i, tile):
+            nc.vector.tensor_copy(tile[:], words[:].bitcast(U32).indirect(offs_sb[:, i * GATHER // 16:(i + 1) * GATHER // 16]))
+            return tile
 
         def products(b, lo, hi):
-            acc = bank(hi - lo)
-            cuts = [lo] + [c for c in CUTS if lo < c < hi] + [hi]
-            for c0, c1 in zip(cuts, cuts[1:]):
-                product(b, c0, c1, acc[:, c0 - lo:c1 - lo])
+            acc = psum.tile([P, hi - lo], F32, name="acc", tag="acc", bufs=8)
+            c0 = lo
+            while c0 < hi:
+                i = c0 // GATHER
+                width = max(w for w in WIDTHS if c0 % w == 0 and c0 + w <= hi)
+                nc.tensor.matmul_mx(
+                    out=acc[:, c0 - lo:c0 - lo + width],
+                    lhsT=weights[b][0][:].bitcast(FP8X4),
+                    lhsT_scale=weights[b][1][:],
+                    rhs=codes[i][:, c0 - i * GATHER:c0 - i * GATHER + width].bitcast(FP8X4),
+                    rhs_scale=x_plane[:, c0:c0 + width],
+                    start=True,
+                    stop=True,
+                )
+                c0 = c0 + width
             return acc
 
-        def gated(b, lo, hi, y):
-            nc.vector.tensor_tensor(y, products(b, lo, hi)[:], gate_sb[:, lo:hi], MULT)
+        def gated(b, lo, hi):
+            nc.vector.tensor_tensor(y[b][:, lo:hi], products(b, lo, hi)[:], gate_sb[:, lo:hi], MULT)
 
-        def scalar_scatter(lo, hi, y):
-            nc.scalar.activation(windows[0][:].indirect(dst_sb[:, lo // 16:hi // 16]), y, COPY)
+        def scalar_scatter(b, lo, hi):
+            nc.scalar.activation(windows[b][:].indirect(dst_sb[:, lo // 16:hi // 16]), y[b][:, lo:hi], COPY)
 
-        def copied(lo, hi, y):
-            nc.vector.tensor_copy(y, products(1, lo, hi)[:])
+        def vector_scatter(b, lo, hi):
+            nc.vector.tensor_tensor(windows[b][:].indirect(dst_sb[:, lo // 16:hi // 16]), y[b][:, lo:hi], gate_sb[:, lo:hi], MULT)
 
-        y0 = keep.tile([P, S], F32, name="y0")
-        y1 = keep.tile([P, S], F32, name="y1")
-
-        codes = [gather_words(i, keep.tile([P, 256], U32, name=f"x_codes{i}", align_bytes=64)) for i in range(2)]
-        grouped0 = interleave_shared(raw0, keep.tile([P, P, PACK], BF16, name="w_grouped0", align_bytes=64))
-        weights = [quantize_weights(0, grouped0)]
-        codes.append(gather_words(2, reuse.tile([P, 256], U32, name="x_codes2", offset=8192, align_bytes=64)))
-        gated(0, 0, P, y0[:, 0:P])
-        gated(0, P, 256, y0[:, P:256])
-        grouped1 = interleave_shared(raw1, keep.tile([P, P, PACK], BF16, name="w_grouped1", align_bytes=64))
-        scalar_scatter(0, 256, y0[:, 0:256])
-        weights.append(quantize_weights(1, grouped1))
-        gated(0, 256, 640, y0[:, 256:640])
-        codes.append(gather_words(3, reuse.tile([P, 256], U32, name="x_codes3", offset=0, align_bytes=64)))
-        scalar_scatter(256, 640, y0[:, 256:640])
-        copied(0, 512, y1[:, 0:512])
-        copied(512, 1024, y1[:, 512:1024])
-        gated(0, 640, 1024, y0[:, 640:1024])
-        scalar_scatter(640, 1024, y0[:, 640:1024])
+        codes = [gather(i, keep.tile([P, GATHER], U32, name=f"x_codes{i}", align_bytes=64)) for i in range(2)]
+        weights = [quantize(0, interleave(0, raw0))]
+        codes.append(gather(2, reuse.tile([P, GATHER], U32, name="x_codes2", offset=8192, align_bytes=64)))
+        gated(0, 0, P)
+        gated(0, P, FIRST)
+        grouped1 = interleave(1, raw1)
+        scalar_scatter(0, 0, HEAD)
+        weights.append(quantize(1, grouped1))
+        codes.append(gather(3, reuse.tile([P, GATHER], U32, name="x_codes3", offset=0, align_bytes=64)))
+        gated(0, FIRST, 3 * GATHER)
+        gated(1, 0, LONG)
+        scalar_scatter(1, 0, LONG)
+        gated(0, 3 * GATHER, S)
+        gated(1, LONG, TAIL)
+        nc.vector.tensor_copy(windows[0][:].indirect(dst_sb[:, HEAD // 16:S // 16]), y[0][:, HEAD:S])
         nc.sync.dma_start(out[0:P, :], windows[0][:])
-
-        nc.vector.tensor_tensor(windows[1][:].indirect(dst_sb[:]), y1[:], gate_sb[:], MULT)
+        nc.scalar.copy(y[1][:, TAIL:S], products(1, TAIL, S)[:])
+        scalar_scatter(1, LONG, TAIL)
+        vector_scatter(1, TAIL, S)
         nc.sync.dma_start(out[P:N, :], windows[1][:])

@@ -19,9 +19,9 @@ ADD = mybir.AluOpType.add
 COPY = mybir.ActivationFunctionType.Copy
 
 GATHER = 256
-FIRST = 256
+FIRST = 320
 HEAD = 256
-LONG = 384
+LONG = 320
 TAIL = 704
 SEED = 64
 ROW0 = 112
@@ -39,11 +39,11 @@ def tile_picked_route2_linnone_p_kernel(tc, x_words, x_scales, gate, w1, offs, d
         offs_sb = keep.tile([P, S // 16], U16, name="offs_sb")
         dst_sb = keep.tile([P, S // 16], U16, name="dst_sb")
         windows = [keep.tile([P, U], F32, name=f"window{b}") for b in range(2)]
-        scales = reuse.tile([P, T], U8, name="scales", offset=0, align_bytes=64)
+        scales = reuse.tile([P, T], U8, name="scales", offset=4096, align_bytes=64)
         x_plane = keep.tile([P, S], U8, name="x_plane", align_bytes=64)
         words = keep.tile([P, T], I32, name="words", align_bytes=64)
         picked = keep.tile([P, S], U8, name="picked", align_bytes=64)
-        y = [keep.tile([P, S], F32, name=f"y{b}") for b in range(2)]
+        y = [keep.tile([P, width], F32, name=f"y{b}") for b, width in enumerate((HEAD, S))]
         w_rows = w1.rearrange("(p j) m -> p j m", j=PACK)
 
         nc.vector.memset(windows[0][:, 0:SEED], 0.0)
@@ -51,7 +51,7 @@ def tile_picked_route2_linnone_p_kernel(tc, x_words, x_scales, gate, w1, offs, d
         nc.scalar.dma_start(scales[ROW0:P, :].bitcast(I32), x_scales[0].bitcast(I32))
         nc.sync.dma_start(offs_sb[:], offs)
         nc.sync.dma_start(words[:], x_words[0].rearrange("p c t -> p (c t)").bitcast(I32))
-        raw0 = reuse.tile([P, PACK, P], F32, name="w_raw0", offset=8192, align_bytes=64)
+        raw0 = reuse.tile([P, PACK, P], F32, name="w_raw0", offset=10240, align_bytes=64)
         nc.sync.dma_start(raw0[:], w_rows[:, :, 0:P])
         nc.sync.dma_start(dst_sb[:], dst)
         nc.vector.memset(x_plane[:].bitcast(I32), 0)
@@ -65,8 +65,8 @@ def tile_picked_route2_linnone_p_kernel(tc, x_words, x_scales, gate, w1, offs, d
         nc.vector.tensor_copy(picked[:], scales[:].indirect(offs_sb[:]))
         for r in range(4):
             nc.sync.dma_start(x_plane[r:P:32, :].bitcast(I32), picked[ROW0 + r:P:4, :].bitcast(I32))
-        raw1 = reuse.tile([P, PACK, P], F32, name="w_raw1", offset=0, align_bytes=64)
-        gate_sb = reuse.tile([P, S], F32, name="gate_sb", offset=2048, align_bytes=64)
+        raw1 = reuse.tile([P, PACK, P], F32, name="w_raw1", offset=3072, align_bytes=64)
+        gate_sb = reuse.tile([P, S], F32, name="gate_sb", offset=5120, align_bytes=64)
         nc.sync.dma_start(raw1[:], w_rows[:, :, P:N])
         nc.sync.dma_start(gate_sb[:, 0:FIRST], gate[:, 0:FIRST])
         nc.sync.dma_start(gate_sb[:, FIRST:S], gate[:, FIRST:S])
@@ -111,26 +111,27 @@ def tile_picked_route2_linnone_p_kernel(tc, x_words, x_scales, gate, w1, offs, d
         def scalar_scatter(b, lo, hi):
             nc.scalar.activation(windows[b][:].indirect(dst_sb[:, lo // 16:hi // 16]), y[b][:, lo:hi], COPY)
 
-        def vector_scatter(b, lo, hi):
-            nc.vector.tensor_tensor(windows[b][:].indirect(dst_sb[:, lo // 16:hi // 16]), y[b][:, lo:hi], gate_sb[:, lo:hi], MULT)
+        def vector_scatter(b, lo, hi, values):
+            nc.vector.tensor_tensor(windows[b][:].indirect(dst_sb[:, lo // 16:hi // 16]), values, gate_sb[:, lo:hi], MULT)
 
         codes = [gather(i, keep.tile([P, GATHER], U32, name=f"x_codes{i}", align_bytes=64)) for i in range(2)]
         weights = [quantize(0, interleave(0, raw0))]
-        codes.append(gather(2, reuse.tile([P, GATHER], U32, name="x_codes2", offset=8192, align_bytes=64)))
+        codes.append(gather(2, reuse.tile([P, GATHER], U32, name="x_codes2", offset=10240, align_bytes=64)))
         gated(0, 0, P)
-        gated(0, P, FIRST)
+        gated(0, P, HEAD)
         grouped1 = interleave(1, raw1)
         scalar_scatter(0, 0, HEAD)
         weights.append(quantize(1, grouped1))
-        codes.append(gather(3, reuse.tile([P, GATHER], U32, name="x_codes3", offset=0, align_bytes=64)))
-        gated(0, FIRST, 3 * GATHER)
+        codes.append(gather(3, reuse.tile([P, GATHER], U32, name="x_codes3", offset=4096, align_bytes=64)))
+        y_rest = reuse.tile([P, S - HEAD], F32, name="y_rest", offset=1024, align_bytes=64)
+        nc.vector.tensor_copy(y_rest[:, 0:3 * GATHER - HEAD], products(0, HEAD, 3 * GATHER)[:])
         gated(1, 0, LONG)
         scalar_scatter(1, 0, LONG)
-        gated(0, 3 * GATHER, S)
+        nc.vector.tensor_copy(y_rest[:, 3 * GATHER - HEAD:S - HEAD], products(0, 3 * GATHER, S)[:])
         gated(1, LONG, TAIL)
-        nc.vector.tensor_copy(windows[0][:].indirect(dst_sb[:, HEAD // 16:S // 16]), y[0][:, HEAD:S])
+        vector_scatter(0, HEAD, S, y_rest[:])
         nc.sync.dma_start(out[0:P, :], windows[0][:])
         nc.scalar.copy(y[1][:, TAIL:S], products(1, TAIL, S)[:])
         scalar_scatter(1, LONG, TAIL)
-        vector_scatter(1, TAIL, S)
+        vector_scatter(1, TAIL, S, y[1][:, TAIL:S])
         nc.sync.dma_start(out[P:N, :], windows[1][:])

@@ -25,7 +25,8 @@ LONG = 320
 TAIL = 704
 SEED = 64
 ROW0 = 112
-SHARE = 80
+SHARE0 = 96
+SHARE1 = 32
 WIDTHS = (256, 128, 64)
 
 
@@ -43,7 +44,7 @@ def tile_picked_route2_linnone_p_kernel(tc, x_words, x_scales, gate, w1, offs, d
         x_plane = keep.tile([P, S], U8, name="x_plane", align_bytes=64)
         words = keep.tile([P, T], I32, name="words", align_bytes=64)
         picked = keep.tile([P, S], U8, name="picked", align_bytes=64)
-        y = [keep.tile([P, width], F32, name=f"y{b}") for b, width in enumerate((HEAD, S))]
+        y = [reuse.tile([P, HEAD], F32, name="y_head", offset=12288, align_bytes=64), keep.tile([P, TAIL], F32, name="y_b")]
         w_rows = w1.rearrange("(p j) m -> p j m", j=PACK)
 
         nc.vector.memset(windows[0][:, 0:SEED], 0.0)
@@ -51,9 +52,12 @@ def tile_picked_route2_linnone_p_kernel(tc, x_words, x_scales, gate, w1, offs, d
         nc.scalar.dma_start(scales[ROW0:P, :].bitcast(I32), x_scales[0].bitcast(I32))
         nc.sync.dma_start(offs_sb[:], offs)
         nc.sync.dma_start(words[:], x_words[0].rearrange("p c t -> p (c t)").bitcast(I32))
-        raw0 = reuse.tile([P, PACK, P], F32, name="w_raw0", offset=10240, align_bytes=64)
-        nc.sync.dma_start(raw0[:], w_rows[:, :, 0:P])
-        nc.sync.dma_start(dst_sb[:], dst)
+        low = keep.tile([P, 2, N], F32, name="w_low", align_bytes=64)
+        nc.sync.dma_start(low[:], w_rows[:, 0:2, :])
+        high0 = reuse.tile([P, 2, P], F32, name="w_high0", offset=10240, align_bytes=64)
+        nc.sync.dma_start(high0[:], w_rows[:, 2:4, 0:P])
+        gate_sb = keep.tile([P, S], F32, name="gate_sb", align_bytes=64)
+        nc.sync.dma_start(gate_sb[:, 0:FIRST], gate[:, 0:FIRST])
         nc.vector.memset(x_plane[:].bitcast(I32), 0)
 
         def spread_zeros(part, width):
@@ -65,17 +69,21 @@ def tile_picked_route2_linnone_p_kernel(tc, x_words, x_scales, gate, w1, offs, d
         nc.vector.tensor_copy(picked[:], scales[:].indirect(offs_sb[:]))
         for r in range(4):
             nc.sync.dma_start(x_plane[r:P:32, :].bitcast(I32), picked[ROW0 + r:P:4, :].bitcast(I32))
-        raw1 = reuse.tile([P, PACK, P], F32, name="w_raw1", offset=3072, align_bytes=64)
-        gate_sb = reuse.tile([P, S], F32, name="gate_sb", offset=5120, align_bytes=64)
-        nc.sync.dma_start(raw1[:], w_rows[:, :, P:N])
-        nc.sync.dma_start(gate_sb[:, 0:FIRST], gate[:, 0:FIRST])
+        high1 = reuse.tile([P, 2, P], F32, name="w_high1", offset=3584, align_bytes=64)
+        nc.sync.dma_start(high1[:], w_rows[:, 2:4, P:N])
+        nc.sync.dma_start(dst_sb[:], dst)
         nc.sync.dma_start(gate_sb[:, FIRST:S], gate[:, FIRST:S])
 
-        def interleave(b, raw):
-            grouped = keep.tile([P, P, PACK], BF16, name=f"w_grouped{b}", align_bytes=64)
-            nc.scalar.copy(grouped[:, 0:SHARE, :].rearrange("p (c i) j -> p c j i", i=4), raw[:, :, 0:SHARE].rearrange("p j (c i) -> p c j i", i=4))
-            nc.gpsimd.tensor_scalar(grouped[:, SHARE:P, :].rearrange("p (c i) j -> p c j i", i=4), raw[:, :, SHARE:P].rearrange("p j (c i) -> p c j i", i=4), 1.0, 0.0, MULT, ADD)
-            return grouped
+        grouped = [keep.tile([P, P, PACK], BF16, name="w_grouped0", align_bytes=64), reuse.tile([P, P, PACK], BF16, name="w_grouped1", offset=9728, align_bytes=64)]
+
+        def by_fours(b, j0, raw, lo, hi):
+            return (grouped[b][:, lo:hi, j0:j0 + 2].rearrange("p (c i) j -> p c j i", i=4), raw[:, :, lo:hi].rearrange("p j (c i) -> p c j i", i=4))
+
+        def on_scalar(b, j0, raw, lo, hi):
+            nc.scalar.copy(*by_fours(b, j0, raw, lo, hi))
+
+        def on_gpsimd(b, j0, raw, lo, hi):
+            nc.gpsimd.tensor_scalar(*by_fours(b, j0, raw, lo, hi), 1.0, 0.0, MULT, ADD)
 
         def quantize(b, grouped):
             w_codes = keep.tile([P, P], U32, name=f"w_codes{b}", align_bytes=64)
@@ -88,7 +96,7 @@ def tile_picked_route2_linnone_p_kernel(tc, x_words, x_scales, gate, w1, offs, d
             return tile
 
         def products(b, lo, hi):
-            acc = psum.tile([P, hi - lo], F32, name="acc", tag="acc", bufs=8)
+            acc = psum.tile([P, hi - lo], F32, name="acc", tag=f"acc{b}_{0 if (b, lo) == (1, TAIL) else lo}", bufs=1)
             c0 = lo
             while c0 < hi:
                 i = c0 // GATHER
@@ -115,23 +123,30 @@ def tile_picked_route2_linnone_p_kernel(tc, x_words, x_scales, gate, w1, offs, d
             nc.vector.tensor_tensor(windows[b][:].indirect(dst_sb[:, lo // 16:hi // 16]), values, gate_sb[:, lo:hi], MULT)
 
         codes = [gather(i, keep.tile([P, GATHER], U32, name=f"x_codes{i}", align_bytes=64)) for i in range(2)]
-        weights = [quantize(0, interleave(0, raw0))]
-        codes.append(gather(2, reuse.tile([P, GATHER], U32, name="x_codes2", offset=10240, align_bytes=64)))
+        on_scalar(0, 0, low[:, :, 0:P], 0, P)
+        on_scalar(0, 2, high0[:], 0, SHARE0)
+        on_gpsimd(0, 2, high0[:], SHARE0, P)
+        weights = [quantize(0, grouped[0])]
+        codes.append(gather(2, reuse.tile([P, GATHER], U32, name="x_codes2", offset=10752, align_bytes=64)))
         gated(0, 0, P)
         gated(0, P, HEAD)
-        grouped1 = interleave(1, raw1)
+        middle_a = products(0, HEAD, 3 * GATHER)
+        on_scalar(1, 0, low[:, :, P:N], 0, P)
+        on_scalar(1, 2, high1[:], 0, SHARE1)
+        on_gpsimd(1, 2, high1[:], SHARE1, P)
         scalar_scatter(0, 0, HEAD)
-        weights.append(quantize(1, grouped1))
+        weights.append(quantize(1, grouped[1]))
         codes.append(gather(3, reuse.tile([P, GATHER], U32, name="x_codes3", offset=4096, align_bytes=64)))
         y_rest = reuse.tile([P, S - HEAD], F32, name="y_rest", offset=1024, align_bytes=64)
-        nc.vector.tensor_copy(y_rest[:, 0:3 * GATHER - HEAD], products(0, HEAD, 3 * GATHER)[:])
         gated(1, 0, LONG)
         scalar_scatter(1, 0, LONG)
+        nc.vector.tensor_copy(y_rest[:, 0:3 * GATHER - HEAD], middle_a[:])
         nc.vector.tensor_copy(y_rest[:, 3 * GATHER - HEAD:S - HEAD], products(0, 3 * GATHER, S)[:])
         gated(1, LONG, TAIL)
         vector_scatter(0, HEAD, S, y_rest[:])
         nc.sync.dma_start(out[0:P, :], windows[0][:])
-        nc.scalar.copy(y[1][:, TAIL:S], products(1, TAIL, S)[:])
+        y_tail = reuse.tile([P, S - TAIL], F32, name="y_tail", offset=12288, align_bytes=64)
+        nc.scalar.copy(y_tail[:], products(1, TAIL, S)[:])
         scalar_scatter(1, LONG, TAIL)
-        vector_scatter(1, TAIL, S, y[1][:, TAIL:S])
+        vector_scatter(1, TAIL, S, y_tail[:])
         nc.sync.dma_start(out[P:N, :], windows[1][:])

@@ -18,15 +18,15 @@ MULT = mybir.AluOpType.mult
 ADD = mybir.AluOpType.add
 COPY = mybir.ActivationFunctionType.Copy
 
-GATHER = 256
-FIRST = 320
+CUTS = (0, 256, 640, 1024)
+FIRST = 384
 HEAD = 256
-LONG = 320
+LONG = 384
 TAIL = 704
 SEED = 64
 ROW0 = 112
 SHARE0 = 96
-SHARE1 = 32
+SHARE1 = 64
 WIDTHS = (256, 128, 64)
 
 
@@ -44,7 +44,7 @@ def tile_picked_route2_linnone_p_kernel(tc, x_words, x_scales, gate, w1, offs, d
         x_plane = keep.tile([P, S], U8, name="x_plane", align_bytes=64)
         words = keep.tile([P, T], I32, name="words", align_bytes=64)
         picked = keep.tile([P, S], U8, name="picked", align_bytes=64)
-        y = [reuse.tile([P, HEAD], F32, name="y_head", offset=12288, align_bytes=64), keep.tile([P, TAIL], F32, name="y_b")]
+        y = [reuse.tile([P, HEAD], F32, name="y_head", offset=12544, align_bytes=64), keep.tile([P, TAIL], F32, name="y_b")]
         w_rows = w1.rearrange("(p j) m -> p j m", j=PACK)
 
         nc.vector.memset(windows[0][:, 0:SEED], 0.0)
@@ -92,20 +92,20 @@ def tile_picked_route2_linnone_p_kernel(tc, x_words, x_scales, gate, w1, offs, d
             return w_codes, w_plane
 
         def gather(i, tile):
-            nc.vector.tensor_copy(tile[:], words[:].bitcast(U32).indirect(offs_sb[:, i * GATHER // 16:(i + 1) * GATHER // 16]))
+            nc.vector.tensor_copy(tile[:], words[:].bitcast(U32).indirect(offs_sb[:, CUTS[i] // 16:CUTS[i + 1] // 16]))
             return tile
 
         def products(b, lo, hi):
             acc = psum.tile([P, hi - lo], F32, name="acc", tag=f"acc{b}_{0 if (b, lo) == (1, TAIL) else lo}", bufs=1)
             c0 = lo
             while c0 < hi:
-                i = c0 // GATHER
-                width = max(w for w in WIDTHS if c0 % w == 0 and c0 + w <= hi)
+                i = max(g for g in range(3) if CUTS[g] <= c0)
+                width = max(w for w in WIDTHS if c0 + w <= min(hi, CUTS[i + 1]))
                 nc.tensor.matmul_mx(
                     out=acc[:, c0 - lo:c0 - lo + width],
                     lhsT=weights[b][0][:].bitcast(FP8X4),
                     lhsT_scale=weights[b][1][:],
-                    rhs=codes[i][:, c0 - i * GATHER:c0 - i * GATHER + width].bitcast(FP8X4),
+                    rhs=codes[i][:, c0 - CUTS[i]:c0 - CUTS[i] + width].bitcast(FP8X4),
                     rhs_scale=x_plane[:, c0:c0 + width],
                     start=True,
                     stop=True,
@@ -122,30 +122,29 @@ def tile_picked_route2_linnone_p_kernel(tc, x_words, x_scales, gate, w1, offs, d
         def vector_scatter(b, lo, hi, values):
             nc.vector.tensor_tensor(windows[b][:].indirect(dst_sb[:, lo // 16:hi // 16]), values, gate_sb[:, lo:hi], MULT)
 
-        codes = [gather(i, keep.tile([P, GATHER], U32, name=f"x_codes{i}", align_bytes=64)) for i in range(2)]
+        codes = [gather(i, keep.tile([P, CUTS[i + 1] - CUTS[i]], U32, name=f"x_codes{i}", align_bytes=64)) for i in range(2)]
         on_scalar(0, 0, low[:, :, 0:P], 0, P)
         on_scalar(0, 2, high0[:], 0, SHARE0)
         on_gpsimd(0, 2, high0[:], SHARE0, P)
         weights = [quantize(0, grouped[0])]
-        codes.append(gather(2, reuse.tile([P, GATHER], U32, name="x_codes2", offset=10752, align_bytes=64)))
+        codes.append(gather(2, reuse.tile([P, S - CUTS[2]], U32, name="x_codes2", offset=10752, align_bytes=64)))
         gated(0, 0, P)
         gated(0, P, HEAD)
-        middle_a = products(0, HEAD, 3 * GATHER)
+        rest_a = [products(0, CUTS[i], CUTS[i + 1]) for i in (1, 2)]
         on_scalar(1, 0, low[:, :, P:N], 0, P)
         on_scalar(1, 2, high1[:], 0, SHARE1)
         on_gpsimd(1, 2, high1[:], SHARE1, P)
         scalar_scatter(0, 0, HEAD)
         weights.append(quantize(1, grouped[1]))
-        codes.append(gather(3, reuse.tile([P, GATHER], U32, name="x_codes3", offset=4096, align_bytes=64)))
         y_rest = reuse.tile([P, S - HEAD], F32, name="y_rest", offset=1024, align_bytes=64)
+        for i in (1, 2):
+            nc.vector.tensor_copy(y_rest[:, CUTS[i] - HEAD:CUTS[i + 1] - HEAD], rest_a[i - 1][:])
         gated(1, 0, LONG)
         scalar_scatter(1, 0, LONG)
-        nc.vector.tensor_copy(y_rest[:, 0:3 * GATHER - HEAD], middle_a[:])
-        nc.vector.tensor_copy(y_rest[:, 3 * GATHER - HEAD:S - HEAD], products(0, 3 * GATHER, S)[:])
         gated(1, LONG, TAIL)
         vector_scatter(0, HEAD, S, y_rest[:])
         nc.sync.dma_start(out[0:P, :], windows[0][:])
-        y_tail = reuse.tile([P, S - TAIL], F32, name="y_tail", offset=12288, align_bytes=64)
+        y_tail = reuse.tile([P, S - TAIL], F32, name="y_tail", offset=12544, align_bytes=64)
         nc.scalar.copy(y_tail[:], products(1, TAIL, S)[:])
         scalar_scatter(1, LONG, TAIL)
         vector_scatter(1, TAIL, S, y_tail[:])

@@ -18,7 +18,7 @@ MULT = mybir.AluOpType.mult
 ADD = mybir.AluOpType.add
 COPY = mybir.ActivationFunctionType.Copy
 
-CUTS = (0, 256, 640, 1024)
+CUTS = (0, 640, 1024)
 FIRST = 384
 HEAD = 256
 LONG = 384
@@ -99,7 +99,7 @@ def tile_picked_route2_linnone_p_kernel(tc, x_words, x_scales, gate, w1, offs, d
             acc = psum.tile([P, hi - lo], F32, name="acc", tag=f"acc{b}_{0 if (b, lo) == (1, TAIL) else lo}", bufs=1)
             c0 = lo
             while c0 < hi:
-                i = max(g for g in range(3) if CUTS[g] <= c0)
+                i = max(g for g in range(2) if CUTS[g] <= c0)
                 width = max(w for w in WIDTHS if c0 + w <= min(hi, CUTS[i + 1]))
                 nc.tensor.matmul_mx(
                     out=acc[:, c0 - lo:c0 - lo + width],
@@ -122,23 +122,23 @@ def tile_picked_route2_linnone_p_kernel(tc, x_words, x_scales, gate, w1, offs, d
         def vector_scatter(b, lo, hi, values):
             nc.vector.tensor_tensor(windows[b][:].indirect(dst_sb[:, lo // 16:hi // 16]), values, gate_sb[:, lo:hi], MULT)
 
-        codes = [gather(i, keep.tile([P, CUTS[i + 1] - CUTS[i]], U32, name=f"x_codes{i}", align_bytes=64)) for i in range(2)]
+        codes = [gather(0, keep.tile([P, CUTS[1]], U32, name="x_codes0", align_bytes=64))]
         on_scalar(0, 0, low[:, :, 0:P], 0, P)
         on_scalar(0, 2, high0[:], 0, SHARE0)
         on_gpsimd(0, 2, high0[:], SHARE0, P)
         weights = [quantize(0, grouped[0])]
-        codes.append(gather(2, reuse.tile([P, S - CUTS[2]], U32, name="x_codes2", offset=10752, align_bytes=64)))
-        gated(0, 0, P)
-        gated(0, P, HEAD)
-        rest_a = [products(0, CUTS[i], CUTS[i + 1]) for i in (1, 2)]
+        codes.append(gather(1, reuse.tile([P, S - CUTS[1]], U32, name="x_codes1", offset=10752, align_bytes=64)))
+        gated(0, 0, HEAD)
+        pieces = ((HEAD, CUTS[1]), (CUTS[1], S))
+        rest_a = [products(0, lo, hi) for lo, hi in pieces]
         on_scalar(1, 0, low[:, :, P:N], 0, P)
         on_scalar(1, 2, high1[:], 0, SHARE1)
         on_gpsimd(1, 2, high1[:], SHARE1, P)
         scalar_scatter(0, 0, HEAD)
         weights.append(quantize(1, grouped[1]))
         y_rest = reuse.tile([P, S - HEAD], F32, name="y_rest", offset=1024, align_bytes=64)
-        for i in (1, 2):
-            nc.vector.tensor_copy(y_rest[:, CUTS[i] - HEAD:CUTS[i + 1] - HEAD], rest_a[i - 1][:])
+        for (lo, hi), acc in zip(pieces, rest_a):
+            nc.vector.tensor_copy(y_rest[:, lo - HEAD:hi - HEAD], acc[:])
         gated(1, 0, LONG)
         scalar_scatter(1, 0, LONG)
         gated(1, LONG, TAIL)

@@ -25,8 +25,8 @@ LONG = 384
 TAIL = 704
 SEED = 64
 ROW0 = 112
-SHARE0 = 96
-SHARE1 = 64
+SHARE0 = 80
+SHARE1 = 80
 WIDTHS = (256, 128, 64)
 
 

@@ -22,7 +22,7 @@ CUTS = (0, 640, 1024)
 FIRST = 384
 HEAD = 256
 LONG = 384
-TAIL = 704
+TAIL = 768
 SEED = 64
 ROW0 = 112
 SHARE0 = 80

@@ -52,8 +52,8 @@ def tile_picked_route2_linnone_p_kernel(tc, x_words, x_scales, gate, w1, offs, d
         nc.scalar.dma_start(scales[ROW0:P, :].bitcast(I32), x_scales[0].bitcast(I32))
         nc.sync.dma_start(offs_sb[:], offs)
         nc.sync.dma_start(words[:], x_words[0].rearrange("p c t -> p (c t)").bitcast(I32))
-        low = keep.tile([P, 2, N], F32, name="w_low", align_bytes=64)
-        nc.sync.dma_start(low[:], w_rows[:, 0:2, :])
+        low = keep.tile([P, 3, P], F32, name="w_low", align_bytes=64)
+        nc.sync.dma_start(low[:].rearrange("p a m -> p (a m)"), w_rows.rearrange("p j m -> p (j m)")[:, 0:3 * P])
         high0 = reuse.tile([P, 2, P], F32, name="w_high0", offset=10240, align_bytes=64)
         nc.sync.dma_start(high0[:], w_rows[:, 2:4, 0:P])
         gate_sb = keep.tile([P, S], F32, name="gate_sb", align_bytes=64)
@@ -69,15 +69,15 @@ def tile_picked_route2_linnone_p_kernel(tc, x_words, x_scales, gate, w1, offs, d
         nc.vector.tensor_copy(picked[:], scales[:].indirect(offs_sb[:]))
         for r in range(4):
             nc.sync.dma_start(x_plane[r:P:32, :].bitcast(I32), picked[ROW0 + r:P:4, :].bitcast(I32))
-        high1 = reuse.tile([P, 2, P], F32, name="w_high1", offset=3584, align_bytes=64)
-        nc.sync.dma_start(high1[:], w_rows[:, 2:4, P:N])
+        high1 = reuse.tile([P, 3, P], F32, name="w_high1", offset=3072, align_bytes=64)
+        nc.sync.dma_start(high1[:], w_rows[:, 1:4, P:N])
         nc.sync.dma_start(dst_sb[:], dst)
         nc.sync.dma_start(gate_sb[:, FIRST:S], gate[:, FIRST:S])
 
         grouped = [keep.tile([P, P, PACK], BF16, name="w_grouped0", align_bytes=64), reuse.tile([P, P, PACK], BF16, name="w_grouped1", offset=9728, align_bytes=64)]
 
         def by_fours(b, j0, raw, lo, hi):
-            return (grouped[b][:, lo:hi, j0:j0 + 2].rearrange("p (c i) j -> p c j i", i=4), raw[:, :, lo:hi].rearrange("p j (c i) -> p c j i", i=4))
+            return (grouped[b][:, lo:hi, j0:j0 + raw.shape[1]].rearrange("p (c i) j -> p c j i", i=4), raw[:, :, lo:hi].rearrange("p j (c i) -> p c j i", i=4))
 
         def on_scalar(b, j0, raw, lo, hi):
             nc.scalar.copy(*by_fours(b, j0, raw, lo, hi))
@@ -123,7 +123,7 @@ def tile_picked_route2_linnone_p_kernel(tc, x_words, x_scales, gate, w1, offs, d
             nc.vector.tensor_tensor(windows[b][:].indirect(dst_sb[:, lo // 16:hi // 16]), values, gate_sb[:, lo:hi], MULT)
 
         codes = [gather(0, keep.tile([P, CUTS[1]], U32, name="x_codes0", align_bytes=64))]
-        on_scalar(0, 0, low[:, :, 0:P], 0, P)
+        on_scalar(0, 0, low[:, 0:3:2, :], 0, P)
         on_scalar(0, 2, high0[:], 0, SHARE0)
         on_gpsimd(0, 2, high0[:], SHARE0, P)
         weights = [quantize(0, grouped[0])]
@@ -131,9 +131,10 @@ def tile_picked_route2_linnone_p_kernel(tc, x_words, x_scales, gate, w1, offs, d
         gated(0, 0, HEAD)
         pieces = ((HEAD, CUTS[1]), (CUTS[1], S))
         rest_a = [products(0, lo, hi) for lo, hi in pieces]
-        on_scalar(1, 0, low[:, :, P:N], 0, P)
-        on_scalar(1, 2, high1[:], 0, SHARE1)
-        on_gpsimd(1, 2, high1[:], SHARE1, P)
+        on_scalar(1, 0, low[:, 1:2, :], 0, SHARE1)
+        on_gpsimd(1, 0, low[:, 1:2, :], SHARE1, P)
+        on_scalar(1, 1, high1[:], 0, SHARE1)
+        on_gpsimd(1, 1, high1[:], SHARE1, P)
         scalar_scatter(0, 0, HEAD)
         weights.append(quantize(1, grouped[1]))
         y_rest = reuse.tile([P, S - HEAD], F32, name="y_rest", offset=1024, align_bytes=64)

@@ -19,7 +19,7 @@ ADD = mybir.AluOpType.add
 COPY = mybir.ActivationFunctionType.Copy
 
 CUTS = (0, 640, 1024)
-FIRST = 384
+FIRST = 256
 HEAD = 256
 LONG = 384
 TAIL = 768

from contextlib import ExitStack

import concourse.mybir as mybir

K, T, S, N, U = 512, 4096, 1024, 256, 2048
P = 128
PACK = 4
FLOPS = 2 * K * N * S

F32 = mybir.dt.float32
BF16 = mybir.dt.bfloat16
I32 = mybir.dt.int32
U32 = mybir.dt.uint32
U16 = mybir.dt.uint16
U8 = mybir.dt.uint8
FP8X4 = mybir.dt.float8_e4m3fn_x4
MULT = mybir.AluOpType.mult
ADD = mybir.AluOpType.add
COPY = mybir.ActivationFunctionType.Copy

CUTS = (0, 640, 1024)
FIRST = 256
HEAD = 256
LONG = 384
TAIL = 768
SEED = 64
ROW0 = 112
SHARE0 = 80
SHARE1 = 80
WIDTHS = (256, 128, 64)


def tile_picked_route2_linnone_p_kernel(tc, x_words, x_scales, gate, w1, offs, dst, out):
    nc = tc.nc
    with ExitStack() as ctx:
        keep = ctx.enter_context(tc.tile_pool(name="keep", bufs=1))
        reuse = ctx.enter_context(tc.tile_pool(name="reuse", bufs=1))
        psum = ctx.enter_context(tc.psum_pool(name="psum", bufs=1))

        offs_sb = keep.tile([P, S // 16], U16, name="offs_sb")
        dst_sb = keep.tile([P, S // 16], U16, name="dst_sb")
        windows = [keep.tile([P, U], F32, name=f"window{b}") for b in range(2)]
        scales = reuse.tile([P, T], U8, name="scales", offset=4096, align_bytes=64)
        x_plane = keep.tile([P, S], U8, name="x_plane", align_bytes=64)
        words = keep.tile([P, T], I32, name="words", align_bytes=64)
        picked = keep.tile([P, S], U8, name="picked", align_bytes=64)
        y = [reuse.tile([P, HEAD], F32, name="y_head", offset=12544, align_bytes=64), keep.tile([P, TAIL], F32, name="y_b")]
        w_rows = w1.rearrange("(p j) m -> p j m", j=PACK)

        nc.vector.memset(windows[0][:, 0:SEED], 0.0)
        nc.vector.memset(scales[0:ROW0, :].bitcast(I32), 0)
        nc.scalar.dma_start(scales[ROW0:P, :].bitcast(I32), x_scales[0].bitcast(I32))
        nc.sync.dma_start(offs_sb[:], offs)
        nc.sync.dma_start(words[:], x_words[0].rearrange("p c t -> p (c t)").bitcast(I32))
        low = keep.tile([P, 3, P], F32, name="w_low", align_bytes=64)
        nc.sync.dma_start(low[:].rearrange("p a m -> p (a m)"), w_rows.rearrange("p j m -> p (j m)")[:, 0:3 * P])
        high0 = reuse.tile([P, 2, P], F32, name="w_high0", offset=10240, align_bytes=64)
        nc.sync.dma_start(high0[:], w_rows[:, 2:4, 0:P])
        gate_sb = keep.tile([P, S], F32, name="gate_sb", align_bytes=64)
        nc.sync.dma_start(gate_sb[:, 0:FIRST], gate[:, 0:FIRST])
        nc.vector.memset(x_plane[:].bitcast(I32), 0)

        def spread_zeros(part, width):
            nc.scalar.copy(part.rearrange("p (a c) -> p a c", c=SEED), windows[0][:, 0:SEED].unsqueeze(1).to_broadcast([P, width // SEED, SEED]))

        spread_zeros(windows[0][:, SEED:U], U - SEED)
        spread_zeros(windows[1][:], U)

        nc.vector.tensor_copy(picked[:], scales[:].indirect(offs_sb[:]))
        for r in range(4):
            nc.sync.dma_start(x_plane[r:P:32, :].bitcast(I32), picked[ROW0 + r:P:4, :].bitcast(I32))
        high1 = reuse.tile([P, 3, P], F32, name="w_high1", offset=3072, align_bytes=64)
        nc.sync.dma_start(high1[:], w_rows[:, 1:4, P:N])
        nc.sync.dma_start(dst_sb[:], dst)
        nc.sync.dma_start(gate_sb[:, FIRST:S], gate[:, FIRST:S])

        grouped = [keep.tile([P, P, PACK], BF16, name="w_grouped0", align_bytes=64), reuse.tile([P, P, PACK], BF16, name="w_grouped1", offset=9728, align_bytes=64)]

        def by_fours(b, j0, raw, lo, hi):
            return (grouped[b][:, lo:hi, j0:j0 + raw.shape[1]].rearrange("p (c i) j -> p c j i", i=4), raw[:, :, lo:hi].rearrange("p j (c i) -> p c j i", i=4))

        def on_scalar(b, j0, raw, lo, hi):
            nc.scalar.copy(*by_fours(b, j0, raw, lo, hi))

        def on_gpsimd(b, j0, raw, lo, hi):
            nc.gpsimd.tensor_scalar(*by_fours(b, j0, raw, lo, hi), 1.0, 0.0, MULT, ADD)

        def quantize(b, grouped):
            w_codes = keep.tile([P, P], U32, name=f"w_codes{b}", align_bytes=64)
            w_plane = keep.tile([P, P], U8, name=f"w_plane{b}", align_bytes=64)
            nc.vector.quantize_mx(out=w_codes[:].bitcast(FP8X4), scales=w_plane[:], in_=grouped[:].rearrange("p m j -> p (m j)"))
            return w_codes, w_plane

        def gather(i, tile):
            nc.vector.tensor_copy(tile[:], words[:].bitcast(U32).indirect(offs_sb[:, CUTS[i] // 16:CUTS[i + 1] // 16]))
            return tile

        def products(b, lo, hi):
            acc = psum.tile([P, hi - lo], F32, name="acc", tag=f"acc{b}_{0 if (b, lo) == (1, TAIL) else lo}", bufs=1)
            c0 = lo
            while c0 < hi:
                i = max(g for g in range(2) if CUTS[g] <= c0)
                width = max(w for w in WIDTHS if c0 + w <= min(hi, CUTS[i + 1]))
                nc.tensor.matmul_mx(
                    out=acc[:, c0 - lo:c0 - lo + width],
                    lhsT=weights[b][0][:].bitcast(FP8X4),
                    lhsT_scale=weights[b][1][:],
                    rhs=codes[i][:, c0 - CUTS[i]:c0 - CUTS[i] + width].bitcast(FP8X4),
                    rhs_scale=x_plane[:, c0:c0 + width],
                    start=True,
                    stop=True,
                )
                c0 = c0 + width
            return acc

        def gated(b, lo, hi):
            nc.vector.tensor_tensor(y[b][:, lo:hi], products(b, lo, hi)[:], gate_sb[:, lo:hi], MULT)

        def scalar_scatter(b, lo, hi):
            nc.scalar.activation(windows[b][:].indirect(dst_sb[:, lo // 16:hi // 16]), y[b][:, lo:hi], COPY)

        def vector_scatter(b, lo, hi, values):
            nc.vector.tensor_tensor(windows[b][:].indirect(dst_sb[:, lo // 16:hi // 16]), values, gate_sb[:, lo:hi], MULT)

        codes = [gather(0, keep.tile([P, CUTS[1]], U32, name="x_codes0", align_bytes=64))]
        on_scalar(0, 0, low[:, 0:3:2, :], 0, P)
        on_scalar(0, 2, high0[:], 0, SHARE0)
        on_gpsimd(0, 2, high0[:], SHARE0, P)
        weights = [quantize(0, grouped[0])]
        codes.append(gather(1, reuse.tile([P, S - CUTS[1]], U32, name="x_codes1", offset=10752, align_bytes=64)))
        gated(0, 0, HEAD)
        pieces = ((HEAD, CUTS[1]), (CUTS[1], S))
        rest_a = [products(0, lo, hi) for lo, hi in pieces]
        on_scalar(1, 0, low[:, 1:2, :], 0, SHARE1)
        on_gpsimd(1, 0, low[:, 1:2, :], SHARE1, P)
        on_scalar(1, 1, high1[:], 0, SHARE1)
        on_gpsimd(1, 1, high1[:], SHARE1, P)
        scalar_scatter(0, 0, HEAD)
        weights.append(quantize(1, grouped[1]))
        y_rest = reuse.tile([P, S - HEAD], F32, name="y_rest", offset=1024, align_bytes=64)
        for (lo, hi), acc in zip(pieces, rest_a):
            nc.vector.tensor_copy(y_rest[:, lo - HEAD:hi - HEAD], acc[:])
        gated(1, 0, LONG)
        scalar_scatter(1, 0, LONG)
        gated(1, LONG, TAIL)
        vector_scatter(0, HEAD, S, y_rest[:])
        nc.sync.dma_start(out[0:P, :], windows[0][:])
        y_tail = reuse.tile([P, S - TAIL], F32, name="y_tail", offset=12544, align_bytes=64)
        nc.scalar.copy(y_tail[:], products(1, TAIL, S)[:])
        scalar_scatter(1, LONG, TAIL)
        vector_scatter(1, TAIL, S, y_tail[:])
        nc.sync.dma_start(out[P:N, :], windows[1][:])
